import numpy as np, ml_dtypes
CORES = [113,118,241,246]
N = 4
BF = ml_dtypes.bfloat16
V, M, S, CAP, P, RO, STEP, LN = 1024, 3584, 256, 64, 10, 3, 310, 2
W1 = 13 * np.arange(16) + 5; W2 = 255 - 14 * np.arange(16); A = N * CAP
def mix(d):
    u = np.add.reduce(W1[:, None] * d, axis=2) & 4095; w = np.add.reduce(W2[:, None] * d, axis=2) & 4095
    return u, (u * w) >> 5
def kid(d, c, hm, t):
    R, n = d.shape[0], d.shape[3]
    hv = np.take_along_axis(hm, d.reshape(R, 8, 1, 16 * n), 3).reshape(R, 8, 16, 16, n)
    e = np.add.reduce(np.minimum(hv, np.abs(c)[:, :, :, None]), axis=2)
    k = np.argmax(e, axis=2); u, h = mix(d); v = (h + 37 * np.max(e, axis=2) + t) & 4095
    void = np.any(d == v[:, :, None], axis=2) | (v >= M)
    new = np.where(np.arange(16)[:, None] == k[:, :, None], v[:, :, None], d)
    q = np.add.reduce((new < v[:, :, None]).astype(np.int64), axis=2)
    return ~void, np.sort(new, axis=2), np.where((((q - k) & 1) == 1)[:, :, None], -(c >> 2), c >> 2)
def spawn(D, C, hm, t):
    start = STEP * (t + 1); a = np.roll(np.any(C != 0, axis=2), -start, axis=2)
    o = np.argsort(~a, axis=2, kind="stable")[:, :, :S]; on = np.take_along_axis(a, o, 2); pl = (o + start) & (V - 1)
    good, ch, c = kid(np.take_along_axis(D, pl[:, :, None], 3), np.take_along_axis(C, pl[:, :, None], 3), hm, t)
    return pl, on, on & good, ch, c
def recs(rng, shape):
    return np.sort(rng.integers(0, M - 15, shape), axis=-2) + np.arange(16)[:, None]
def base(rng, share=None):
    lim = rng.choice(np.array([1, 3, 20, 127]), (N, 8, 1, V), p=[0.15, 0.15, 0.2, 0.5]); C = rng.integers(-lim, lim + 1, (N, 8, 16, V))
    if share is None: share = rng.choice(np.array([0.4, 0.55, 0.75, 0.92]), (N, 8, 1, 1))
    C = C * (rng.random((N, 8, 1, V)) < share)
    return recs(rng, (N, 8, 16, V)), C, rng.integers(0, 128, (N, 8, 16, M))
def plant(rng, D, C, hm, part, twin=False, t=0, own=False):
    live = np.any(C != 0, axis=2); pl, on, good, ch, c = spawn(D, C, hm, t); u, h = mix(ch)
    busy = np.zeros((N, 8, V), bool); np.put_along_axis(busy, pl, on, 2)
    q, g, s = np.nonzero(good & (rng.random(good.shape) < part)); r = h[q, g, s] & (N - 1)
    p = ((h[q, g, s] >> LN) + rng.integers(0, P, q.size) * (2 * u[q, g, s] + 1)) & (V - 1)
    one = np.unique((r * 8 + g) * V + p, return_index=True)[1]
    if not own: one = one[~busy[r[one], g[one], p[one]]]
    q, g, s, r, p = q[one], g[one], s[one], r[one], p[one]
    rec = ch[q, g, :, s]; w = c[q, g, :, s]; lv = live[r, g, p][:, None]; bs = busy[r, g, p][:, None]; n = one.size
    if twin:
        nxt = np.concatenate([rec[:, 1:], np.full((n, 1), M)], axis=1); way = rng.random(n)
        fit = (rec[:, :14] + 1 < rec[:, 1:15] - 2) & (rec[:, 2:] + 1 < nxt[:, 2:]); i = np.argmax(fit * (0.01 + rng.random(fit.shape)), axis=1)
        z = np.nonzero(np.any(fit, axis=1) & (way < 0.4))[0]
        rec[z, i[z]] += 1; rec[z, i[z] + 1] -= 2; rec[z, i[z] + 2] += 1
        i = np.where(rng.random(n) < 0.3, 15, rng.integers(0, 16, n))
        z = np.nonzero((way > 0.6) & (rec[np.arange(n), i] + 1 < nxt[np.arange(n), i]))[0]
        rec[z, i[z]] += 1
    D[r, g, :, p] = rec
    mode = rng.integers(0, 4, (n, 1)); old = C[r, g, :, p]; some = np.any(w != 0, axis=1)[:, None]
    new = np.where(lv & (mode == 0) & some, -w, np.where(lv & (mode == 1), np.where(w < 0, -127, 127), old))
    C[r, g, :, p] = np.where(bs & (mode == 3), rng.choice(np.array([-1, 1]), (n, 16)), new)
def pack(D, C, hm):
    return {"det": np.ascontiguousarray((256 * D + C + 128).reshape(N, 128, V)).astype(np.int32), "ham": np.ascontiguousarray(hm.reshape(N, 128, M)).astype(np.float32).astype(BF)}
def setup_inputs(rng):
    D, C, hm = base(rng)
    for t in range(RO - 1, -1, -1): plant(rng, D, C, hm, 0.35, False, t, True)
    return pack(D, C, hm)
def setup_inputs_slots(rng):
    D, C, hm = base(rng, 2.0); C[:, :, 0] = np.where(np.any(C != 0, axis=2), C[:, :, 0], 1)
    for q in range(N):
        good, ch, c = kid(D[q:q + 1], C[q:q + 1], hm[q:q + 1], 0); mine = good[0] & ((mix(ch)[1][0] & (N - 1)) == ((q + 1) & (N - 1)))
        for g in range(8):
            hit = rng.permutation(np.nonzero(mine[g])[0]); rest = rng.permutation(np.nonzero(~mine[g])[0])
            n = min((CAP, CAP + 1, CAP - 1, S, 0, 1, CAP, CAP + 1)[g], len(hit))
            seq = np.concatenate([rng.permutation(np.concatenate([hit[:n], rest[:S - n]])), rng.permutation(np.concatenate([hit[n:], rest[S - n:]]))])
            k = int(rng.integers(S, V - 63)); o = rng.permutation(V); at = (np.concatenate([np.sort(o[:k]), o[k:]]) + STEP) & (V - 1)
            d2 = np.zeros_like(D[q, g]); c2 = np.zeros_like(C[q, g])
            d2[:, at] = D[q, g][:, seq]; c2[:, at[:k]] = C[q, g][:, seq[:k]]; D[q, g] = d2; C[q, g] = c2
    return pack(D, C, hm)
def setup_inputs_ties(rng):
    D, C, hm = base(rng); ev = np.ascontiguousarray(D[:, ::2]); u, h = mix(ev)
    x = np.take_along_axis(ev, rng.integers(0, 16, (N, 4, 1, V)), 2); y = np.take_along_axis(ev, rng.integers(0, 16, (N, 4, 1, V)), 2)
    goal = rng.permuted(np.concatenate([x, x + 1, x - 1, y, y + 1, ev[:, :, :1], ev[:, :, 15:], 0 * x, 0 * x + M - 1, 0 * x + 4095], axis=2), axis=2)
    e = ((goal - h[:, :, None]) * pow(37, -1, 4096)) & 4095; ok = (e >= 1) & (e <= 2032)
    e = np.take_along_axis(e, np.argmax(ok, axis=2)[:, :, None], 2); ok = np.any(ok, axis=2)[:, :, None]
    z = (np.arange(16)[:, None] + rng.integers(0, 16, (N, 4, 1, V))) & 15
    new = ((e >> 4) + (z < (e & 15))) * rng.choice(np.array([-1, 1]), (N, 4, 16, V)); live = np.any(C[:, ::2] != 0, axis=2)[:, :, None]
    C[:, ::2] = np.where(ok & live, new, C[:, ::2])
    hm[:, ::2] = 127; hm[:, 1::2] = rng.choice(np.array([0, 9, 60]), (N, 4, 1, M))
    hm[np.arange(N), 2 * rng.integers(0, 4, N) + 1] = 0
    plant(rng, D, C, hm, 0.2)
    return pack(D, C, hm)
def setup_inputs_twins(rng):
    D, C, hm = base(rng); hm = np.repeat(hm[:1], N, axis=0); ix = rng.integers(0, 40, (N, 8, 1, V))
    pd = np.repeat(recs(rng, (1, 8, 16, 40)), N, axis=0)
    pc = np.repeat(np.where(np.arange(40) < 12, rng.integers(0, 4, (1, 8, 16, 40)), rng.integers(4, 128, (1, 8, 16, 40))), N, axis=0)
    use = rng.random((N, 8, 1, V)) < 0.6; live = np.any(C != 0, axis=2)[:, :, None]
    sign = np.where(rng.random((N, 8, 1, V)) < 0.4, 1, rng.choice(np.array([-1, 1]), (N, 8, 16, V)))
    D = np.where(use, np.take_along_axis(pd, ix, 3), D)
    C = np.where(use & live, np.take_along_axis(pc, ix, 3) * sign, C)
    plant(rng, D, C, hm, 0.5); plant(rng, D, C, hm, 0.4); plant(rng, D, C, hm, 0.4, True)
    return pack(D, C, hm)
def setup_inputs_thin(rng):
    D, C, hm = base(rng, 2.0); lone = np.arange(16)[:, None] == rng.integers(0, 16, (N, 8, 1, V))
    C[:, 1::2] = np.where(lone, np.where(C == 0, -1, C), 0)[:, 1::2]
    C[:, :, 0] = np.where(np.any(C != 0, axis=2), C[:, :, 0], 1); sizes = np.array([0, 1, 5, S - 1, S, S + 1, V - 1, V])
    for q in range(N):
        for g in range(8):
            n = int(sizes[g]) if q == 0 else int(rng.choice(sizes)); o = rng.permutation(V)
            if n == 5: o = np.array([0, V - 1, STEP - 1, STEP, STEP + 1])
            keep = np.zeros(V, np.int64); keep[o[:n]] = 1; C[q, g] = C[q, g] * keep
    plant(rng, D, C, hm, 0.3)
    return pack(D, C, hm)
def setup_inputs_spread(rng):
    D, C, hm = base(rng)
    D = np.sort(((M - 15) * rng.random((N, 8, 16, V)) ** rng.choice(np.array([1.0, 4.0]), (N, 8, 1, V))).astype(np.int64), axis=2) + np.arange(16)[:, None]
    size = np.exp2(7 * rng.random((N, 8, 1, V))); live = np.any(C != 0, axis=2)[:, :, None]
    C = np.minimum((size * rng.random((N, 8, 16, V))).astype(np.int64), 127) * rng.choice(np.array([-1, 1]), (N, 8, 16, V)) * live
    hm = np.minimum((np.exp2(7 * rng.random((N, 8, 1, M))) * rng.random((N, 8, 16, M))).astype(np.int64), 127)
    plant(rng, D, C, hm, 0.3)
    return pack(D, C, hm)
def check_inputs(d):
    bad = []
    x = d["det"].astype(np.int64).reshape(N, 8, 16, V); o = x >> 8
    if np.min(o) < 0 or np.max(o) > M - 1: bad.append("orbitals of det")
    if np.min(x & 255) < 1: bad.append("counts of det")
    if not np.all(o[:, :, 1:] > o[:, :, :-1]): bad.append("rising orbitals of det")
    h = d["ham"].astype(np.float32)
    if not np.all((h >= 0) & (h <= 127) & (h == np.floor(h))): bad.append("numbers of ham")
    return bad
def reference(det, ham):
    x = det.astype(np.int64).reshape(N, 8, 16, V); D = x >> 8; C = (x & 255) - 128
    hm = ham.astype(np.float32).astype(np.int64).reshape(N, 8, 16, M); num = np.arange(P)[:, None]
    for t in range(RO):
        pl, on, good, ch, c = spawn(D, C, hm, t)
        sel = np.zeros((N, 8, V), bool); np.put_along_axis(sel, pl, on, 2)
        C = C - np.sign(C) * sel[:, :, None]
        f = good[:, :, None] & ((mix(ch)[1] & (N - 1))[:, :, None] == np.arange(N)[:, None])
        before = np.add.accumulate(f.astype(np.int64), axis=3) - f.astype(np.int64)
        q, g, r, s = np.nonzero(f & (before < CAP)); a = q * CAP + before[q, g, r, s]
        ad = np.zeros((N, 8, 16, A), np.int64); ac = np.zeros((N, 8, 16, A), np.int64); there = np.zeros((N, 8, A), bool)
        ad[r, g, :, a] = ch[q, g, :, s]; ac[r, g, :, a] = c[q, g, :, s]; there[r, g, a] = True
        u, h = mix(ad)
        p = ((h >> LN)[:, :, None] + num * (2 * u + 1)[:, :, None]) & (V - 1)
        live = np.any(C != 0, axis=2); lp = np.take_along_axis(live, p.reshape(N, 8, P * A), 2).reshape(N, 8, P, A)
        dp = np.take_along_axis(D, p.reshape(N, 8, 1, P * A), 3).reshape(N, 8, 16, P, A)
        same = np.all(dp == ad[:, :, :, None], axis=2) & lp
        score = np.where(same, num, np.where(lp, 2 * P, P + num))
        ok = there & (np.min(score, axis=2) < 2 * P); place = np.take_along_axis(p, np.argmin(score, axis=2)[:, :, None], 2)[:, :, 0]
        r, g, a = np.nonzero(ok); low = np.full((N, 8, V), A); np.minimum.at(low, (r, g, place[r, g, a]), a)
        r, g, a = np.nonzero(ok & (np.take_along_axis(low, place, 2) == np.arange(A))); b = place[r, g, a]
        D[r, g, :, b] = ad[r, g, :, a]; C[r, g, :, b] = np.clip(C[r, g, :, b] + ac[r, g, :, a], -127, 127)
    return {"y": (256 * D + C + 128).reshape(N, 128, V).astype(np.float32)}

@@ -1,0 +1,642 @@
+from concourse.bass import DstId, RemoteDMATransfer
+from concourse.mybir import AluOpType as O, ActivationFunctionType as F
+import math
+
+F32, BF, I32, U16 = "float32", "bfloat16", "int32", "uint16"
+BUFS = {
+    F32: dict(TD=1280, QT=1280, ONE=160, NEGI=128, ZG=24, WT=24, SHP=128, SHN=128, QW=128, QE=128, DM=136, SW=16, SC=2, TRS=16,
+              TRA=16, WX=8, XI=8, THR=1, XJ=1, RC=1, B1=1, B2=1, MC=160, MR=16, PA=24, PB=24, TV=1024, TM=1024, DB=64, RF=64,
+              LM=136, LD=16, LE=16, DF=256, EM=64, EA=256, EB=256, EC=256, ED=256, CH=256, CF32=256, ON=16, OK1=16, SN0=16,
+              K1=64, K2=32, K3=16, K4=16, K5=16, K6=16, FS=16, XF=256, AT=256, AD=256, QA=256, QS=256, ZF=64,
+              ST=16, S1=160, S2=160, S3=160, S4=80, S5=32, S6=16, S7=16, M1=16, M2=16, M3=16, M4=16, NU=16,
+              PW=16, LO=16, YT=1280, YN=256, PR5=1280, BAD=16, SB0=512, SB1=512, SB2=512, IN0=256, IN1=256, IN2=256, PF=32),
+    BF: dict(TC=1280, ham=3584, ONEB=256, G8=8, G16=8, SEL8=8, SELB=8, RW=8, TRI=128, IDB=128, KC=128, C128=128, C64=128,
+             BIGL=128, R8=128, WC=128, WBIG=8, ZW=1280, IM=160, SV0=128, SV1=128, SK0=128, SK1=128, SS0=128, SS1=128, QB=1024,
+             LV=64, OL=1024, OA=1024, OB=1024, BS=1088, AB=256, CN=256, hv=4096, MK=4096, F4B=48, R4=128, SG=256, SNB=16,
+             R5=128, OM=64, CFD=256, ABF=256, XB=1024, CMP=2560, FD=32, R6=128, CO=256, CNW=256, SVX0=128, SVX1=128),
+    I32: dict(DET=1024, CI=1024, PI=16, PJ=1, PK=24, PL=24, R32=64, LOW=64, MX=16, E1=16, E2=16, E3=16, VV=16, F4=48, H1=32,
+              H2=32, HP=16, HV=16, SGI=16, N1=16, N2=16, N3=16, KM2=16, KM1=16, FI=256, I1=32, I2=32, PR=16, OW=16, J1=48,
+              J2=32, JP=16, ZD=64, ZI=160, ZJ=160, HQ=16, PLC=16, DG=32, SL2=16),
+    U16: dict(GU=16, DU=256, OFF=16, ZU=160, PU=256, FO=16),
+}
+SCRATCH, WIDTH, WHERE = {}, {}, {}
+for _d in BUFS:
+    _p = 0
+    for _n, _w in BUFS[_d].items():
+        _n = "hamt" if _n == "ham" else _n
+        WIDTH[_n] = _w
+        if _w <= 160:
+            WHERE[_n] = ("small_" + _d, _p)
+            _p += (_w + 15) // 16 * 16
+        else:
+            SCRATCH[_n] = ("sbuf", [128, _w], _d)
+    if _p:
+        SCRATCH["small_" + _d] = ("sbuf", [128, _p], _d)
+PSUM = ["P%d" % _k for _k in range(7)] + ["TP"]
+for _n in PSUM:
+    WIDTH[_n] = 128 if _n == "TP" else 512
+    SCRATCH[_n] = ("psum", [128, WIDTH[_n]], BF if _n == "TP" else F32)
+SEMAPHORES = ["qv", "qs", "qt", "qg", "ld0", "ld1", "st0", "snd", "rx0", "rx1", "rx2"]
+
+
+def rank_program(g, core, T, topo):
+    me = T.rank_of(core)
+    if me is None:
+        return
+    V, S, PE = g.vector, g.scalar, g.tensor
+    ENG = {"v": V, "s": S, "t": PE, "g": g, "d": g.sync}
+    cnt, known, clk = {"v": 0, "s": 0, "t": 0, "g": 0}, {q: {} for q in ENG}, {}
+    wr, rd, last = {}, {}, {}
+    semof = {"v": ("qv", 1), "s": ("qs", 1), "t": ("qt", 1), "g": ("qg", 1)}
+
+    def w(name, a=0, b=None, st=1, p=128):
+        b = WIDTH[name] if b is None else b
+        n, o = WHERE.get(name, (name, 0))
+        ap = T[n][0:p, o + a:o + b] if st == 1 else T[n][0:p, o + a:o + b:st]
+        m = 0
+        if st == 1:
+            m = ((1 << (b - a)) - 1) << a
+        else:
+            for c in range(a, b, st):
+                m |= 1 << c
+        return (ap, [(name, m)], [])
+
+    def ind(win, off):
+        return (win[0].indirect(off[0]), win[1], off[1])
+
+    def wait(q, q2, k):
+        if known[q].get(q2, 0) >= k:
+            return
+        sem, inc = semof[q2]
+        ENG[q].wait_ge(T.sem[sem], k * inc)
+        for a, n in list(clk.get((q2, k), {}).items()) + [(q2, k)]:
+            if known[q].get(a, 0) < n:
+                known[q][a] = n
+
+    def deps(q, reads, writes):
+        need = {}
+
+        def add(q2, k):
+            if need.get(q2, 0) < k:
+                need[q2] = k
+        for n, m in reads + writes:
+            if n in PSUM:
+                for q2, k in last.get(n, {}).items():
+                    if q2 != q:
+                        add(q2, k)
+        for n, m in reads:
+            for q2, k, m2 in wr.get(n, []):
+                if m & m2:
+                    add(q2, k)
+        for n, m in writes:
+            for q2, k, m2 in wr.get(n, []):
+                if m & m2 and not (q == "t" and q2 == "t"):
+                    add(q2, k)
+            for q2, k, m2 in rd.get(n, []):
+                if m & m2:
+                    add(q2, k)
+        for q2, k in sorted(need.items(), key=lambda x: x[0] == q):
+            wait(q, q2, k)
+
+    def note(q, k, reads, writes):
+        clk[(q, k)] = dict(known[q] if q in known else {})
+        for n, m in writes:
+            wr[n] = [x for x in wr.get(n, []) if x[2] & ~m] + [(q, k, m)]
+            rd[n] = [x for x in rd.get(n, []) if x[2] & ~m]
+        for n, m in reads:
+            rd[n] = [x for x in rd.get(n, []) if not (x[0] == q and not x[2] & ~m)] + [(q, k, m)]
+        for n, m in reads + writes:
+            if n in PSUM:
+                last.setdefault(n, {})[q] = k
+
+    def E(q, f, ins, outs):
+        reads = [r for x in ins for r in x[1] + x[2]] + [r for x in outs for r in x[2]]
+        writes = [r for x in outs for r in x[1]]
+        deps(q, reads, writes)
+        cnt[q] += 1
+        f().then_inc(T.sem[semof[q][0]], 1)
+        note(q, cnt[q], reads, writes)
+
+    def dma(q, out, in_, sem, reads, writes):
+        deps(q, reads, writes)
+        ENG[q].dma_start(out=out, in_=in_).then_inc(T.sem[sem], 16)
+        semof[sem] = (sem, 16)
+        clk[(sem, 1)] = dict(known[q])
+        note(sem, 1, reads, writes)
+
+    def col(x):
+        return [x] if isinstance(x, tuple) else []
+
+    def ap(x):
+        return x[0] if isinstance(x, tuple) else x
+
+    def tt(o, a, b, op):
+        E("v", lambda: V.tensor_tensor(out=o[0], in0=a[0], in1=b[0], op=op), [a, b], [o])
+
+    def ts(o, a, s1, op0, s2=None, op1=None):
+        if op1 is None:
+            E("v", lambda: V.tensor_scalar(out=o[0], in0=a[0], scalar1=ap(s1), scalar2=None, op0=op0), [a] + col(s1), [o])
+        else:
+            E("v", lambda: V.tensor_scalar(out=o[0], in0=a[0], scalar1=ap(s1), scalar2=ap(s2), op0=op0, op1=op1),
+              [a] + col(s1) + col(s2), [o])
+
+    def cp(o, a):
+        E("v", lambda: V.tensor_copy(out=o[0], in_=a[0]), [a], [o])
+
+    def fill(o, c):
+        E("v", lambda: V.memset(o[0], c), [], [o])
+
+    def act(o, a, f=F.Copy, bias=0.0, scale=1.0):
+        E("s", lambda: S.activation(out=o[0], in_=a[0], func=f, bias=ap(bias), scale=ap(scale)), [a] + col(bias) + col(scale), [o])
+
+    def mm(o, l, r, start=True, stop=True):
+        E("t", lambda: PE.matmul(out=o[0], lhsT=l[0], rhs=r[0], start=start, stop=stop), [l, r], [o])
+
+    def tr(o, a):
+        E("t", lambda: PE.transpose(out=o[0], in_=a[0], identity=w("IDB")[0]), [a, w("IDB")], [o])
+
+    def iota(o, pat, base, cm):
+        E("g", lambda: g.iota(o[0], pattern=pat, base=base, channel_multiplier=cm, allow_small_or_imprecise_dtypes=True), [], [o])
+
+    def aff(o, a, pat, op, base, cm):
+        E("g", lambda: g.affine_select(out=o[0], in_=a[0], pattern=pat, compare_op=op, fill=0.0, base=base, channel_multiplier=cm),
+          [a], [o])
+
+    dma("d", T["DET"][:, :], T.det[:, :], "ld0", [], [("DET", (1 << 1024) - 1)])
+    dma("s", T["hamt"][:, :], T.ham[:, :], "ld1", [], [("hamt", (1 << 3584) - 1)])
+
+    fill(w("ONEB"), 1.0)
+    fill(w("ONE"), 1.0)
+    fill(w("NEGI"), -1.0)
+    fill(w("QE"), 4096.0)
+    fill(w("C64"), 64.0)
+    iota(w("PI"), [[-1, 16]], 16, 1)
+    iota(w("PJ"), [[0, 1]], 0, 1)
+    aff(w("G8"), w("ONEB", 0, 8), [[-16, 8]], O.is_ge, 0, 1)
+    aff(w("G8"), w("G8"), [[16, 8]], O.is_ge, 15, -1)
+    for t in range(3):
+        iota(w("PK", 8 * t, 8 * t + 8), [[128, 8]], 310 * (t + 1), 1)
+    aff(w("TRI"), w("ONEB", 0, 128), [[1, 128]], O.is_ge, -1, -1)
+    iota(w("SW"), [[16, 16]], -1024, 0)
+    aff(w("DM"), w("ONE", 0, 136), [[-16, 8], [0, 17]], O.is_ge, 0, 1)
+    aff(w("DM"), w("DM"), [[16, 8], [0, 17]], O.is_ge, 15, -1)
+    aff(w("IDB"), w("ONEB", 0, 128), [[-1, 128]], O.is_equal, 0, 1)
+    aff(w("QE"), w("QE"), [[-16, 8], [-2, 16]], O.is_equal, 0, 1)
+    aff(w("QW"), w("ONE", 0, 128), [[-16, 8], [-2, 16]], O.is_equal, -1, 1)
+    tt(w("QW"), w("QW"), w("QE"), O.add)
+    aff(w("QW"), w("QW"), [[0, 8], [-1, 16]], O.is_ge, 7, 0)
+    aff(w("SHP"), w("ONE", 0, 128), [[1, 128]], O.is_equal, -1, -1)
+    aff(w("SHN"), w("ONE", 0, 128), [[1, 128]], O.is_equal, 1, -1)
+    iota(w("KC"), [[-1, 16], [0, 8]], 15, 0)
+    iota(w("SC"), [[128, 2]], 0, 1)
+    iota(w("WT", 0, 8), [[-208, 8]], 5, 13)
+    iota(w("WT", 8, 16), [[224, 8]], 255, -14)
+    aff(w("WT", 0, 16), w("WT", 0, 16), [[0, 2], [-16, 8]], O.is_ge, 0, 1)
+    aff(w("WT", 0, 16), w("WT", 0, 16), [[0, 2], [16, 8]], O.is_ge, 15, -1)
+    aff(w("WT", 16, 24), w("ONE", 0, 8), [[-16, 8]], O.is_equal, -15, 1)
+    ts(w("PL"), w("PK"), 255, O.bitwise_and)
+    ts(w("PA"), w("PL"), 0.5, O.mult)
+    ts(w("PL"), w("PK"), 768, O.bitwise_and)
+    ts(w("PB"), w("PL"), -2048.0, O.add, 0.5, O.mult)
+    ts(w("PI"), w("PI"), 15, O.bitwise_and)
+    ts(w("MR"), w("PI"), 0.0, O.is_equal)
+    ts(w("PJ"), w("PJ"), 15, O.bitwise_and)
+    cp(w("RC"), w("PJ"))
+    ts(w("SW"), w("SW"), w("RC"), O.add)
+    aff(w("NEGI"), w("NEGI"), [[-1, 128]], O.is_equal, 0, 1)
+    for h in range(2):
+        aff(w("SV%d" % h), w("C64"), [[-2, 8], [0, 16]], O.is_equal, -h, 1)
+        aff(w("SK%d" % h), w("ONEB", 0, 128), [[-2, 8], [0, 16]], O.is_equal, -32 - h, 1)
+        aff(w("SS%d" % h), w("ONEB", 0, 128), [[-2, 8], [0, 16]], O.is_equal, -h, 1)
+
+    MAG = 12582912.0
+    START = [310 * (t + 1) & 1023 for t in range(3)]
+
+    def rot(t, a, b):
+        s, cut = START[t], 1024 - START[t]
+        out = []
+        if a < cut:
+            out.append((a, min(b, cut), a + s))
+        if b > cut:
+            out.append((max(a, cut), b, max(a, cut) - cut))
+        return out
+
+    for c in (0, 512):
+        ts(w("CI", c, c + 512), w("DET", c, c + 512), 255, O.bitwise_and)
+        ts(w("TC", c, c + 512), w("CI", c, c + 512), -128.0, O.add)
+    for a, b in ((0, 202), (202, 714), (714, 1024)):
+        for x, y, p in rot(0, a, b):
+            act(w("QB", x, y), w("TC", p, p + y - x), F.Abs)
+    for c in (0, 512):
+        ts(w("TV", c, c + 512), w("DET", c, c + 512), -128.0, O.add, 1 / 256, O.mult)
+        act(w("TM", c, c + 512), w("TV", c, c + 512), F.Identity, MAG)
+        act(w("TD", c, c + 512), w("TM", c, c + 512), F.Identity, -MAG)
+    fill(w("SHP", 0, 128, 16), 0.0)
+    fill(w("SHN", 15, 128, 16), 0.0)
+    fill(w("BIGL"), 0.0)
+    fill(w("BIGL", 15, 128, 16), 64.0)
+    fill(w("C128"), 1 / 128)
+    fill(w("TC", 1024, 1280), 0.0)
+    fill(w("TD", 1024, 1280), 0.0)
+    fill(w("ZG"), 0.0)
+    cp(w("ZG", 8, 16), w("G8"))
+    ts(w("G16"), w("G8"), 16.0, O.mult)
+    SEL = [w("ZG", 8, 24), w("ZG", 0, 16)]
+
+    for h in range(2):
+        aff(w("SVX%d" % h), w("ONEB", 0, 128), [[-2, 8], [0, 16]], O.is_equal, -16 - h, 1)
+    iota(w("TRS"), [[0, 8], [128, 2]], 256, 1)
+    iota(w("TRA"), [[0, 8], [128, 2]], 1024, 1)
+    iota(w("MC"), [[1, 10], [0, 16]], 20, 0)
+    iota(w("IM"), [[1, 10], [0, 16]], 0, 0)
+    iota(w("XI"), [[16, 8]], 0, 0)
+    iota(w("XJ"), [[0, 1]], 0, 1)
+    aff(w("SEL8"), w("ONEB", 0, 8), [[-16, 8]], O.is_equal, -8, 1)
+    aff(w("RW"), w("G8"), [[16, 8]], O.is_ge, 7, -1)
+    for h in range(2):
+        z = w("ZW", 640 * h + 160, 640 * h + 320)
+        aff(z, w("ONEB", 0, 160), [[0, 10], [-16, 16]], O.is_ge, 128 * h, 1)
+        aff(z, z, [[0, 10], [16, 16]], O.is_ge, 15 - 128 * h, -1)
+
+    def late_constants():
+        for h in range(2):
+            tt(w("SV%d" % h), w("SV%d" % h), w("SVX%d" % h), O.add)
+        fill(w("R8"), 0.0)
+        cp(w("R8", 8, 128, 16), w("G8"))
+        ts(w("B1"), w("RC"), -8192.0, O.mult, 8192.0 * 15 + 4096, O.add)
+        ts(w("B2"), w("RC"), 8192.0, O.mult, 4096 - 8192.0 * 15, O.add)
+        for t in range(3):
+            fill(w("SB%d" % t, 0, 256), 0.0)
+
+    def last_constants():
+        ts(w("SELB"), w("SEL8"), 16.0, O.mult)
+        tt(w("RW"), w("RW"), w("SELB"), O.add)
+        for h in range(2):
+            z = [w("ZW", 640 * h + 160 * f, 640 * h + 160 * f + 160) for f in range(4)]
+            ts(z[0], z[1], 32.0, O.mult)
+            tt(z[3], z[1], w("IM"), O.mult)
+            ts(z[2], z[3], 32.0, O.mult)
+        ts(w("XI"), w("XI"), w("RC"), O.add)
+        L3 = math.log(3.0)
+        ts(w("XI"), w("XI"), -L3, O.mult, 55 * L3, O.add)
+        ts(w("XJ"), w("XJ"), -L3, O.mult, 55 * L3, O.add)
+        act(w("WX"), w("XI"), F.Exp)
+        act(w("THR"), w("XJ"), F.Exp)
+        ts(w("THR"), w("THR"), 2.2, O.mult)
+        for c in range(8):
+            ts(w("WC", 8 * c, 8 * c + 8), w("G8"), w("WX", c, c + 1), O.mult)
+        ts(w("WBIG"), w("G8"), 1e29, O.mult)
+
+    def t2w(src, n, X):
+        for r in range(16):
+            if r % 2:
+                act(w(X, r, 16 * n, 16), src, F.Copy, 0.0, w("MR", r, r + 1))
+            else:
+                ts(w(X, r, 16 * n, 16), src, w("MR", r, r + 1), O.mult)
+
+    peers = [q for q in range(4) if q != me]
+    near = [q for q in peers if T.cores[q] in topo.cores_of(core)]
+    far = [q for q in peers if q not in near]
+
+    def send(t):
+        sb, plan, used = "SB%d" % t, [], []
+        for i, q in enumerate(far):
+            e = topo.engines(core, T.cores[q])
+            k = len(e) // len(far)
+            plan.append((q, e[i * k:(i + 1) * k]))
+            used += e[i * k:(i + 1) * k]
+        for i, q in enumerate(near):
+            e = [x for x in topo.engines(core, T.cores[q]) if x not in used]
+            k = len(e) // len(near)
+            plan.append((q, e[i * k:(i + 1) * k]))
+        got = sum(len(e) for q, e in plan)
+        deps("g", w(sb, 0, 256)[1], [])
+        tf = []
+        for q, e in plan:
+            rid, pid = topo.addr(T.cores[q], core)
+            tf.append(RemoteDMATransfer(dst_ids=[DstId(rid=rid, pnc=pid)], dma_engine_mask=sum(1 << x for x in e),
+                                        remote_sem=T.sem["rx%d" % t], src=T[sb][:, 64 * q:64 * q + 64],
+                                        dst=T["IN%d" % t][:, 64 * me:64 * me + 64], alu_op=0))
+        g.remote_dma_fused(tf, local_sem=T.sem["snd"])
+        rx = "rx%d" % t
+        semof[rx] = (rx, got)
+        note(rx, 1, [], [r for q in peers for r in w("IN%d" % t, 64 * q, 64 * q + 64)[1]])
+        act(w("IN%d" % t, 64 * me, 64 * me + 64), w(sb, 64 * me, 64 * me + 64))
+        return got
+
+    def first_qt(b):
+        mm(w("P6", 0, 512), w("QW"), w("TD", 512 * b, 512 * b + 512), True, False)
+        parts = [(0, 310, 714), (310, 512, 0)] if b == 0 else [(0, 512, 202)]
+        for i, (x, y, p) in enumerate(parts):
+            mm(w("P6", x, y), w("R8"), w("QB", p, p + y - x), False, i == len(parts) - 1)
+        act(w("QT", 512 * b, 512 * b + 512), w("P6", 0, 512))
+
+    sent = 0
+    for t in range(3):
+        IN, SB = "IN%d" % t, "SB%d" % t
+        if t:
+            for i, (a, b) in enumerate(((0, 256), (256, 512), (512, 768), (768, 1024))):
+                for x, y, p in rot(t, a, b):
+                    if i % 2:
+                        cp(w("QB", x, y), w("QT", p, p + y - x))
+                    else:
+                        act(w("QB", x, y), w("QT", p, p + y - x))
+        for k in range(8):
+            mm(w("P0", 8 * k, 8 * k + 8), w("QB", 128 * k, 128 * k + 128), w("SEL8") if t else w("G8"))
+        ts(w("LV"), w("P0", 0, 64), 0.0, O.is_gt)
+        ts(w("DB"), w("P0", 0, 64), 0.0, O.is_equal, 4096.0, O.mult)
+        mm(w("P1", 0, 64), w("TRI"), w("LV"), True, False)
+        for d in range(1, 8):
+            mm(w("P1", 8 * d, 64), w("ONEB", 0, 128), w("LV", 0, 64 - 8 * d), False, d == 7)
+        tt(w("RF"), w("P1", 0, 64), w("DB"), O.add)
+        cp(w("R32"), w("RF"))
+        ts(w("LOW"), w("R32"), 15, O.bitwise_and)
+        for h in range(17):
+            act(w("BS", h, 1088, 17), w("RF"), F.Sign, 0.5 - 16 * h)
+        if t == 0:
+            late_constants()
+        for l in range(16):
+            ts(w("OL", l, 1024, 16), w("LOW"), float(l), O.is_equal)
+        for k in range(8):
+            c = (128 * k, 128 * k + 128)
+            ts(w("OA", *c), w("OL", *c), w("PA", 8 * t + k, 8 * t + k + 1), O.mult)
+            act(w("OB", *c), w("OL", *c), F.Copy, 0.0, w("PB", 8 * t + k, 8 * t + k + 1))
+        for k in range(8):
+            for i, n in enumerate(("OA", "OB")):
+                mm(w("P2", 0, 136), w(n, 128 * k, 128 * k + 128), w("BS", 136 * k, 136 * k + 136), k + i == 0, k + i == 8)
+        for k in range(8):
+            mm(w("P0", 0, 8), w("ONEB", 0, 128), w("LV", 8 * k, 8 * k + 8), k == 0, k == 7)
+        if t:
+            cp(ind(w("TD"), w("FO")), w("AD"))
+        tt(w("LM"), w("P2", 0, 136), w("DM"), O.mult)
+        for n in (68, 34, 17):
+            tt(w("LM", 0, n), w("LM", 0, n), w("LM", n, 2 * n), O.add)
+        tt(w("LD"), w("LM", 0, 16), w("LM", 1, 17), O.subtract)
+        tt(w("LE"), w("LD"), w("SW"), O.min)
+        ts(w("GU"), w("LE"), 2048.0, O.add)
+        act(w("AB"), ind(w("TC"), w("GU")), F.Abs)
+        mm(w("P3", 0, 256), w("IDB"), w("AB"))
+        cp(w("DU"), ind(w("TD"), w("GU")))
+        CUT = [0, 64, 128, 192, 256]
+
+        def look(a, b):
+            return w("hv", 16 * a, 16 * b), ind(w("hamt"), w("DU", a, b))
+        for j in range(1, 4):
+            act(*look(CUT[j], CUT[j + 1]))
+        act(w("CN"), ind(w("TC"), w("GU")))
+        cp(w("DF"), w("DU"))
+        cp(*look(CUT[0], CUT[1]))
+        for h in range(2):
+            mm(w("P0", 64 + h, 96, 2), w("DF", 128 * h, 128 * h + 128), w("WT", 0, 16))
+
+        def mins(a, b):
+            for k in range(16):
+                tt(w("MK", 256 * k + a, 256 * k + b), w("hv", 16 * a + k, 16 * b, 16), w("P3", a, b), O.min)
+
+        def tree(h):
+            p = "P%d" % (1 + h)
+            mm(w(p, 0, 128), w("C128"), w("KC"), True, False)
+            for k in range(16):
+                mm(w(p, 8 * k, 8 * k + 8), w("MK", 256 * k + 128 * h, 256 * k + 128 * h + 128), w("G16"), False, k == 15)
+
+        def top(h):
+            p, o = "P%d" % (1 + h), 128 * h
+            cp(w("EM"), w(p, 64, 128))
+            tt(w("EA", o, o + 64), w(p, 0, 64), w("EM"), O.max)
+            for n in (32, 16):
+                tt(w("EA", o, o + n), w("EA", o, o + n), w("EA", o + n, o + 2 * n), O.max)
+            tt(w("MX", h, 16, 2), w("EA", o, o + 8), w("EA", o + 8, o + 16), O.max)
+        mm(w("P4", 0, 256), w("SHP"), w("DF"))
+        mm(w("P4", 256, 512), w("SHN"), w("DF"), True, False)
+        mm(w("P4", 256, 512), w("BIGL"), w("ONEB"), False, True)
+        mm(w("P5", 0, 256), w("NEGI"), w("DF"), True, False)
+        if t == 0:
+            first_qt(0)
+        mins(0, CUT[2])
+        tree(0)
+        mins(CUT[2], CUT[3])
+        for h in range(2):
+            ts(w("ON", h, 16, 2), w("P0", 0, 8), w("SC", h, h + 1), O.is_gt)
+        cp(w("H1"), w("P0", 64, 96))
+        ts(w("H2"), w("H1"), 4095, O.bitwise_and)
+        tt(w("HP"), w("H2", 0, 16), w("H2", 16, 32), O.mult)
+        ts(w("HP"), w("HP"), 5, O.arith_shift_right)
+        ts(w("HV"), w("HP"), float(t), O.add)
+        top(0)
+        mins(CUT[3], CUT[4])
+        tree(1)
+        top(1)
+        ts(w("F4", 32, 48), w("MX"), 15, O.bitwise_and)
+        ts(w("E1"), w("MX"), 4, O.arith_shift_right)
+        ts(w("E2"), w("E1"), 37.0, O.mult)
+        tt(w("E3"), w("E2"), w("HV"), O.add)
+        ts(w("F4", 0, 16), w("E3"), 6, O.arith_shift_right, 63, O.bitwise_and)
+        ts(w("F4", 16, 32), w("E3"), 63, O.bitwise_and)
+        cp(w("F4B"), w("F4"))
+        tr(w("TP", 0, 128, 1, 48), w("F4B"))
+        r4 = w("R4", 0, 128, 1, 48)
+        cp(r4, w("TP", 0, 128, 1, 48))
+        for h in range(2):
+            mm(w("P6", 256 + 128 * h, 384 + 128 * h), w("SK%d" % h, 0, 128, 1, 48), r4)
+        for h in range(2):
+            mm(w("P6", 128 * h, 128 * h + 128), w("SV%d" % h, 0, 128, 1, 48), r4)
+        for h in range(2):
+            mm(w("P5", 128 * h, 128 * h + 128), w("SV%d" % h, 0, 128, 1, 48), r4, False, h == 1)
+        act(w("P0", 0, 256), w("P6", 256, 512), F.Relu, w("B2"), 8192.0)
+        act(w("P1", 0, 256), w("P6", 256, 512), F.Relu, w("B1"), -8192.0)
+        act(w("SG"), w("P5", 0, 256), F.Sign)
+        ts(w("FI"), w("CN"), 0.25, O.mult, -0.375, O.add)
+        ts(w("KM2"), w("F4", 32, 48), 2.0, O.mult)
+        ts(w("KM1"), w("F4", 32, 48), 1.0, O.add)
+        ts(w("VV"), w("E3"), 4095, O.bitwise_and)
+        ts(w("OK1"), w("VV"), 3584.0, O.is_lt)
+        tt(w("OK1"), w("OK1"), w("ON"), O.mult)
+        tt(w("EA"), w("DF"), w("P0", 0, 256), O.add)
+        tt(w("EB"), w("EA"), w("P6", 0, 256), O.min)
+        tt(w("EC"), w("EB"), w("P4", 256, 512), O.min)
+        tt(w("ED"), w("DF"), w("P1", 0, 256), O.subtract)
+        tt(w("EA"), w("EC"), w("P4", 0, 256), O.max)
+        tt(w("CH"), w("EA"), w("ED"), O.max)
+        for h in range(2):
+            mm(w("P3", h, 16, 2), w("SG", 128 * h, 128 * h + 128), w("G8"))
+        for h in range(2):
+            mm(w("P2", h, 32, 2), w("CH", 128 * h, 128 * h + 128), w("WT", 0, 16))
+        act(w("P4", 0, 256), w("CH"), F.Copy, 0.0, 256.0)
+        cp(w("SGI"), w("P3", 0, 16))
+        tt(w("N1"), w("SGI"), w("KM2"), O.add)
+        ts(w("N2"), w("N1"), 14.0, O.is_gt)
+        ts(w("N1"), w("SGI"), 1, O.arith_shift_right)
+        tt(w("N3"), w("N1"), w("N2"), O.add)
+        tt(w("N2"), w("N3"), w("KM1"), O.add)
+        ts(w("N1"), w("N2"), 1, O.bitwise_and)
+        ts(w("SNB"), w("N1"), -2.0, O.mult, 1.0, O.add)
+        tr(w("TP", 0, 128, 1, 16), w("SNB"))
+        ts(w("N3"), w("SGI"), 1, O.bitwise_and)
+        ts(w("SN0"), w("N3"), 0.0, O.is_equal)
+        tt(w("OK1"), w("OK1"), w("SN0"), O.mult)
+        ts(w("BAD"), w("OK1"), -8.0, O.mult, 8.0, O.add)
+        cp(w("R5", 0, 128, 1, 16), w("TP", 0, 128, 1, 16))
+        for h in range(2):
+            mm(w("P0", 128 * h, 128 * h + 128), w("SS%d" % h, 0, 128, 1, 16), w("R5", 0, 128, 1, 16))
+        cp(w("I1"), w("P2", 0, 32))
+        ts(w("I2"), w("I1"), 4095, O.bitwise_and)
+        tt(w("PR"), w("I2", 0, 16), w("I2", 16, 32), O.mult)
+        ts(w("OW"), w("PR"), 5, O.arith_shift_right, 3, O.bitwise_and)
+        tt(w("K3"), w("OW"), w("BAD"), O.add)
+        for q in range(4):
+            ts(w("OM", 16 * q, 16 * q + 16), w("K3"), float(q), O.is_equal)
+        mm(w("P5", 0, 64), w("TRI"), w("OM"), True, False)
+        for q in range(4):
+            mm(w("P5", 16 * q + 1, 16 * q + 16, 2), w("ONEB", 0, 128), w("OM", 16 * q, 16 * q + 16, 2), False, q == 3)
+        tt(w("CF32"), w("FI"), w("P0", 0, 256), O.mult)
+        tt(w("K1"), w("P5", 0, 64), w("OM"), O.mult)
+        tt(w("K2"), w("K1", 0, 32), w("K1", 32, 64), O.add)
+        tt(w("K4"), w("K2", 0, 16), w("K2", 16, 32), O.add)
+        ts(w("K5"), w("K4"), 64.0, O.is_ge, 1024.0, O.mult)
+        ts(w("K6"), w("K3"), 64.0, O.mult)
+        tt(w("K6"), w("K6"), w("K4"), O.add)
+        tt(w("K5"), w("K5"), w("K6"), O.add)
+        for h in range(2):
+            tt(w("FS", 8 * h, 8 * h + 8), w("K5", h, 16, 2), w("TRS", h, 16, 2), O.min)
+        t2w(w("FS"), 16, "XF")
+        for h in range(2):
+            mm(w("P6", 0, 16), w("XF", 128 * h, 128 * h + 128), SEL[h], h == 0, h == 1)
+        tt(w("ED"), w("CF32"), w("P4", 0, 256), O.add)
+        cp(w("OFF"), w("P6", 0, 16))
+        cp(ind(w(SB), w("OFF")), w("ED"))
+        sent += send(t)
+        act(w("P3", 256, 512), w("CN"), F.Sign)
+        if t == 0:
+            first_qt(1)
+        tt(w("CFD"), w("CN"), w("P3", 256, 512), O.subtract)
+        act(w("ABF"), w("CFD"), F.Abs)
+        mm(w("P0", 0, 256), w("QW"), w("DF"), True, False)
+        mm(w("P0", 0, 256), w("R8"), w("ABF"), False, True)
+        act(w("QS"), w("P0", 0, 256))
+        cp(ind(w("TC"), w("GU")), w("CFD"))
+        if t == 0:
+            last_constants()
+        cp(ind(w("QT"), w("GU")), w("QS"))
+        if t == 2:
+            for b in range(2):
+                act(w("P5", 0, 512), w("TD", 512 * b, 512 * b + 512), F.Copy, 128.0, 256.0)
+                tt(w("YT", 512 * b, 512 * b + 512), w("P5", 0, 512), w("TC", 512 * b, 512 * b + 512), O.add)
+        ts(w("AT", 0, 128), w(IN, 0, 128), 1 / 256, O.mult, MAG, O.add)
+        act(w("AT", 128, 256), w(IN, 128, 256), F.Identity, MAG, 1 / 256)
+        ts(w("AD", 0, 128), w("AT", 0, 128), -MAG, O.add)
+        act(w("AD", 128, 256), w("AT", 128, 256), F.Identity, -MAG)
+        for h in range(2):
+            mm(w("P1", h, 48, 2), w("AD", 128 * h, 128 * h + 128), w("WT"))
+        mm(w("P2", 0, 256), w("QW"), w("AD"))
+        act(w("P6", 0, 256), w("AD"), F.Copy, 0.0, -256.0)
+        cp(w("J1"), w("P1", 0, 48))
+        ts(w("J2"), w("J1", 0, 32), 4095, O.bitwise_and)
+        tt(w("JP"), w("J2", 0, 16), w("J2", 16, 32), O.mult)
+        ts(w("ZD", 32, 48), w("J2", 0, 16), 4, O.arith_shift_right, 31, O.bitwise_and)
+        ts(w("SL2"), w("J2", 0, 16), 15, O.bitwise_and)
+        ts(w("ZD", 0, 16), w("JP"), 12, O.arith_shift_right, 31, O.bitwise_and)
+        ts(w("ZD", 16, 32), w("JP"), 7, O.arith_shift_right, 31, O.bitwise_and)
+        ts(w("ZD", 48, 64), w("SL2"), 2.0, O.mult, 1.0, O.add)
+        for h in range(2):
+            cp(w("ZF", 32 * h, 32 * h + 32), w("ZD", h, 64, 2))
+        t2w(w("ZF"), 64, "XB")
+        act(w("QA"), w("P2", 0, 256))
+        ts(w("HQ"), w("JP"), 7, O.arith_shift_right, 1023, O.bitwise_and)
+        ts(w("ST"), w("J2", 0, 16), 2.0, O.mult, 1.0, O.add)
+        ts(w("NU"), w("J1", 32, 48), 1.0, O.is_lt, 40.0, O.mult)
+        tt(w("P6", 0, 256), w(IN), w("P6", 0, 256), O.add)
+        for c in range(2):
+            for h in range(2):
+                for f in range(4):
+                    mm(w("P%d" % (3 + c), 0, 80), w("XB", (32 * h + 8 * f) * 16, (32 * h + 8 * f) * 16 + 128),
+                       w("ZW", 640 * h + 160 * f + 80 * c, 640 * h + 160 * f + 80 * c + 80), h + f == 0, h + f == 4)
+            z = (80 * c, 80 * c + 80)
+            cp(w("ZI", *z), w("P%d" % (3 + c), 0, 80))
+            ts(w("ZJ", *z), w("ZI", *z), 1023, O.bitwise_and)
+            cp(w("ZU", *z), w("ZJ", *z))
+
+        def probe(m):
+            o = w("CMP", 256 * m, 256 * m + 256)
+            if m < 5:
+                tt(o, ind(w("QT", 0, 1024), w("ZU", 16 * m, 16 * m + 16)), w("QA"), O.is_equal)
+            else:
+                tt(o, w("PR5", 256 * (m - 5), 256 * (m - 4)), w("P2", 0, 256), O.is_equal)
+            for h in range(2):
+                mm(w("P%d" % (5 if m < 5 else 0), 16 * (m % 5) + h, 16 * (m % 5) + 16, 2),
+                   w("CMP", 256 * m + 128 * h, 256 * m + 128 * h + 128), w("RW"))
+
+        def score(c):
+            p, z = w("P%d" % (0 if c else 5), 0, 80), (80 * c, 80 * c + 80)
+            ts(w("S1", *z), p, 8.0, O.is_equal, -10.0, O.mult)
+            ts(w("S2", *z), p, 8.0, O.is_ge, -10.0, O.mult)
+            tt(w("S3", *z), w("S1", *z), w("S2", *z), O.add)
+            tt(w("S1", *z), w("S3", *z), w("MC", *z), O.add)
+        for m in range(5):
+            act(w("PR5", 256 * m, 256 * m + 256), ind(w("QT", 0, 1024), w("ZU", 16 * m + 80, 16 * m + 96)))
+        for m in range(6):
+            probe(m)
+        score(0)
+        for m in range(6, 10):
+            probe(m)
+        score(1)
+        tt(w("S4"), w("S1", 0, 80), w("S1", 80, 160), O.min)
+        tt(w("S5"), w("S4", 0, 32), w("S4", 32, 64), O.min)
+        tt(w("S6"), w("S5", 0, 16), w("S5", 16, 32), O.min)
+        tt(w("S7"), w("S6"), w("S4", 64, 80), O.min)
+        ts(w("M1"), w("S7"), 10.0, O.is_ge, -10.0, O.mult)
+        tt(w("M2"), w("M1"), w("S7"), O.add)
+        tt(w("M3"), w("M2"), w("ST"), O.mult)
+        tt(w("S6"), w("S7"), w("NU"), O.add)
+        ts(w("M4"), w("S6"), 20.0, O.is_ge, 2048.0, O.mult)
+        tt(w("N1"), w("M3"), w("HQ"), O.add)
+        ts(w("N2"), w("N1"), 1023, O.bitwise_and)
+        tt(w("PLC"), w("N2"), w("M4"), O.add)
+        ts(w("DG", 0, 16), w("PLC"), 6, O.arith_shift_right)
+        ts(w("DG", 16, 32), w("PLC"), 63, O.bitwise_and)
+        cp(w("FD"), w("DG"))
+        tr(w("TP", 0, 128, 1, 32), w("FD"))
+        for h in range(2):
+            cp(w("PF", 8 * h, 8 * h + 8), w("PLC", h, 16, 2))
+        cp(w("R6", 0, 128, 1, 32), w("TP", 0, 128, 1, 32))
+        for h in range(2):
+            mm(w("P0", 128 * h, 128 * h + 128), w("SV%d" % h, 0, 128, 1, 32), w("R6", 0, 128, 1, 32))
+        t2w(w("PF", 0, 16), 16, "XF")
+        for h in range(2):
+            mm(w("P1", 0, 16), w("XF", 128 * h, 128 * h + 128), SEL[h], h == 0, h == 1)
+        cp(w("PU"), w("P0", 0, 256))
+        cp(w("PW"), w("P1", 0, 16))
+        for c in range(16):
+            a = 0 if c < 8 else 128
+            ts(w("MK", 256 * c + a, 256 * c + 256), w("PU", a, 256), w("PW", c, c + 1), O.is_equal)
+            wc = w("WC", 8 * (c % 8), 8 * (c % 8) + 8)
+            if c < 8:
+                mm(w("P3", 0, 16, 2), w("MK", 256 * c, 256 * c + 128), wc, c == 0, c == 7)
+            mm(w("P4", 1, 16, 2), w("MK", 256 * c + 128, 256 * c + 256), wc if c > 7 else w("WBIG"), c == 0, c == 15)
+        for h in range(2):
+            ts(w("LO", h, 16, 2), w("P%d" % (3 + h), h, 16, 2), w("THR"), O.is_ge, 4096.0, O.mult)
+        tt(w("M1"), w("LO"), w("PLC"), O.add)
+        for h in range(2):
+            tt(w("PF", 16 + 8 * h, 24 + 8 * h), w("M1", h, 16, 2), w("TRA", h, 16, 2), O.min)
+        t2w(w("PF", 16, 32), 16, "XF")
+        for h in range(2):
+            mm(w("P5", 0, 16), w("XF", 128 * h, 128 * h + 128), SEL[h], h == 0, h == 1)
+        cp(w("FO"), w("P5", 0, 16))
+        act(w("CO"), ind(w("TC"), w("FO")))
+        if t == 2:
+            act(w("P1", 0, 256), w("AD"), F.Copy, 128.0, 256.0)
+        tt(w("EB"), w("CO"), w("P6", 0, 256), O.add)
+        ts(w("CNW"), w("EB"), 127.0, O.min, -127.0, O.max)
+        if t < 2:
+            act(w("ABF"), w("CNW"), F.Abs)
+            mm(w("P2", 0, 256), w("R8"), w("ABF"))
+            cp(ind(w("TC"), w("FO")), w("CNW"))
+            tt(w("QS"), w("QA"), w("P2", 0, 256), O.add)
+            cp(ind(w("QT"), w("FO")), w("QS"))
+        else:
+            tt(w("YN"), w("CNW"), w("P1", 0, 256), O.add)
+            cp(ind(w("YT"), w("FO")), w("YN"))
+            dma("d", T.y[:, :], T["YT"][:, 0:1024], "st0", w("YT", 0, 1024)[1], [])
+    wait("d", "st0", 1)
+    g.wait_ge(T.sem.snd, sent)
+    for q in ("v", "s", "t", "g"):
+        wait("g", q, cnt[q])

@@ -2,22 +2,25 @@ from concourse.bass import DstId, RemoteDMATransfer
 from concourse.mybir import AluOpType as O, ActivationFunctionType as F
 import math
 
-F32, BF, I32, U16 = "float32", "bfloat16", "int32", "uint16"
+WAKE, SLACK = 0.10, 0.05
+F32, BF, I32, U16, F16 = "float32", "bfloat16", "int32", "uint16", "float16"
 BUFS = {
     F32: dict(TD=1280, QT=1280, ONE=160, NEGI=128, ZG=24, WT=24, SHP=128, SHN=128, QW=128, QE=128, DM=136, SW=16, SC=2, TRS=16,
-              TRA=16, WX=8, XI=8, THR=1, XJ=1, RC=1, B1=1, B2=1, MC=160, MR=16, PA=24, PB=24, TV=1024, TM=1024, DB=64, RF=64,
-              LM=136, LD=16, LE=16, DF=256, EM=64, EA=256, EB=256, EC=256, ED=256, CH=256, CF32=256, ON=16, OK1=16, SN0=16,
-              K1=64, K2=32, K3=16, K4=16, K5=16, K6=16, FS=16, XF=256, AT=256, AD=256, QA=256, QS=256, ZF=64,
-              ST=16, S1=160, S2=160, S3=160, S4=80, S5=32, S6=16, S7=16, M1=16, M2=16, M3=16, M4=16, NU=16,
-              PW=16, LO=16, YT=1280, YN=256, PR5=1280, BAD=16, SB0=512, SB1=512, SB2=512, IN0=256, IN1=256, IN2=256, PF=32),
-    BF: dict(TC=1280, ham=3584, ONEB=256, G8=8, G16=8, SEL8=8, SELB=8, RW=8, TRI=128, IDB=128, KC=128, C128=128, C64=128,
-             BIGL=128, R8=128, WC=128, WBIG=8, ZW=1280, IM=160, SV0=128, SV1=128, SK0=128, SK1=128, SS0=128, SS1=128, QB=1024,
-             LV=64, OL=1024, OA=1024, OB=1024, BS=1088, AB=256, CN=256, hv=4096, MK=4096, F4B=48, R4=128, SG=256, SNB=16,
-             R5=128, OM=64, CFD=256, ABF=256, XB=1024, CMP=2560, FD=32, R6=128, CO=256, CNW=256, SVX0=128, SVX1=128),
-    I32: dict(DET=1024, CI=1024, PI=16, PJ=1, PK=24, PL=24, R32=64, LOW=64, MX=16, E1=16, E2=16, E3=16, VV=16, F4=48, H1=32,
-              H2=32, HP=16, HV=16, SGI=16, N1=16, N2=16, N3=16, KM2=16, KM1=16, FI=256, I1=32, I2=32, PR=16, OW=16, J1=48,
-              J2=32, JP=16, ZD=64, ZI=160, ZJ=160, HQ=16, PLC=16, DG=32, SL2=16),
-    U16: dict(GU=16, DU=256, OFF=16, ZU=160, PU=256, FO=16),
+              TRA=16, WX=8, XI=8, THR=1, XJ=1, RC=1, B1=1, B2=1, MC=160, MR=16, PA=24, TV=1024, TM=1024, DB=64, RF=64,
+              LM=136, LD=16, DF=256, EM=64, EU=64, ET=256, EB=256, EC=256, ED=256, DP=256, DN=256, CH=256, CF32=256, ON=16,
+              OK1=16, SN0=16, K1=64, K2=32, K3=16, K4=16, K5=16, K6=16, K7=16, K8=16, FS=16, XF=256, AT=256, AD=256, QA=256,
+              QS=256, QN=256, CV=256, ZF=64, ST=16, S1=160, S2=160, S3=160, S4=80, S5=32, S6=16, S7=16, SN=16, M1=16, M3=16,
+              M4=16, M5=16, NU=16, PW=16, LO=16, YT=1280, YN=256, PR5=1536, BAD=16, SB0=512, SB1=512, SB2=512, IN0=256,
+              IN1=256, IN2=256, PF=32),
+    BF: dict(TC=1280, ham=3584, ONEB=256, G8=8, G16=8, SEL8=8, SELB=8, RW=8, TRI=128, IDB=128, IDN=128, KC=128, KD=136, C128=128,
+             C64=128, BIGL=128, R8=128, WC=128, WBIG=8, ZW=1280, IM=160, SV0=128, SV1=128, SK0=128, SK1=128, SS0=128, SS1=128,
+             QB=1024, LV=64, OL=1024, BS=1088, AB=256, CN=256, hv=4096, MK=4096, F4B=48, R4=128, SG=256, SNB=16, R5=128, OM=64,
+             CFD=256, ABF=256, ABN=256, XB=1024, CMP=2560, FD=32, R6=128, CO=256, CNW=256, SVX0=128, SVX1=128),
+    I32: dict(DET=1024, CI=1024, PI=16, PJ=1, PK=24, PL=24, R32=64, LOW=64, MX=16, E1=16, E3=16, VV=16, F4=48, H1=32,
+              H2=32, HP=16, HV=16, SGI=16, N1=16, N2=16, N3=16, N4=16, N5=16, N6=16, N7=16, KM2=16, KM1=16, FI=256, I1=32, I2=32,
+              PR=16, OW=16, J1=48, J2=32, JP=16, ZD=64, ZI=160, ZJ=160, HQ=16, ST0=16, PN=16, PM=16, PLC=16, DG=32, SL2=16),
+    F16: dict(OA=1024),
+    U16: dict(GU=16, DU=256, OFF=16, ZU=160, PU=256, PO=16, FO=16),
 }
 SCRATCH, WIDTH, WHERE = {}, {}, {}
 for _d in BUFS:
@@ -32,6 +35,7 @@ for _d in BUFS:
             SCRATCH[_n] = ("sbuf", [128, _w], _d)
     if _p:
         SCRATCH["small_" + _d] = ("sbuf", [128, _p], _d)
+TWO = list(BUFS[F16]) + list(BUFS[BF]) + list(BUFS[U16])
 PSUM = ["P%d" % _k for _k in range(7)] + ["TP"]
 for _n in PSUM:
     WIDTH[_n] = 128 if _n == "TP" else 512
@@ -62,7 +66,7 @@ def rank_program(g, core, T, topo):
         return (ap, [(name, m)], [])
 
     def ind(win, off):
-        return (win[0].indirect(off[0]), win[1], off[1])
+        return (win[0].indirect(off[0]), win[1], off[1], 16 * off[1][0][1].bit_count())
 
     def wait(q, q2, k):
         if known[q].get(q2, 0) >= k:
@@ -109,20 +113,92 @@ def rank_program(g, core, T, topo):
             if n in PSUM:
                 last.setdefault(n, {})[q] = k
 
-    def E(q, f, ins, outs):
+    calls = []
+
+    def wide(x):
+        return x[3] if len(x) > 3 else x[1][0][1].bit_count()
+
+    def E(q, f, ins, outs, cost):
+        def emit(reads, writes):
+            deps(q, reads, writes)
+            cnt[q] += 1
+            f().then_inc(T.sem[semof[q][0]], 1)
+            note(q, cnt[q], reads, writes)
         reads = [r for x in ins for r in x[1] + x[2]] + [r for x in outs for r in x[2]]
-        writes = [r for x in outs for r in x[1]]
-        deps(q, reads, writes)
-        cnt[q] += 1
-        f().then_inc(T.sem[semof[q][0]], 1)
-        note(q, cnt[q], reads, writes)
+        for x in ins + outs:
+            if len(x) > 3:
+                reads = reads + x[2]
+        calls.append((q, emit, reads, [r for x in outs for r in x[1]], cost, 0.0))
 
     def dma(q, out, in_, sem, reads, writes):
-        deps(q, reads, writes)
-        ENG[q].dma_start(out=out, in_=in_).then_inc(T.sem[sem], 16)
-        semof[sem] = (sem, 16)
-        clk[(sem, 1)] = dict(known[q])
-        note(sem, 1, reads, writes)
+        def emit(reads, writes):
+            deps(q, reads, writes)
+            ENG[q].dma_start(out=out, in_=in_).then_inc(T.sem[sem], 16)
+            semof[sem] = (sem, 16)
+            clk[(sem, 1)] = dict(known[q])
+            note(sem, 1, reads, writes)
+        calls.append((q, emit, reads, writes, 0.1, 5.0))
+
+    def schedule():
+        n = len(calls)
+        succ, npred = [[] for _ in range(n)], [0] * n
+        W, R, B = {}, {}, {}
+        for j, (q, emit, reads, writes, cost, lat) in enumerate(calls):
+            pred = {}
+
+            def edge(i, wk):
+                pred[i] = max(pred.get(i, 0.0), wk)
+            for nm, m in reads + writes:
+                if nm in PSUM:
+                    for q2, i in B.get(nm, {}).items():
+                        edge(i, 0.0 if q2 == q else WAKE)
+            for nm, m in reads:
+                for i, m2 in W.get(nm, []):
+                    if m & m2:
+                        edge(i, WAKE)
+            for nm, m in writes:
+                for i, m2 in W.get(nm, []) + R.get(nm, []):
+                    if m & m2:
+                        edge(i, 0.0 if q == calls[i][0] == "t" else WAKE)
+            for i, wk in pred.items():
+                succ[i].append((j, wk))
+            npred[j] = len(pred)
+            for nm, m in writes:
+                W[nm] = [x for x in W.get(nm, []) if x[1] & ~m] + [(j, m)]
+                R[nm] = [x for x in R.get(nm, []) if x[1] & ~m]
+            for nm, m in reads:
+                R.setdefault(nm, []).append((j, m))
+            for nm, m in reads + writes:
+                if nm in PSUM:
+                    B.setdefault(nm, {})[q] = j
+        way = [0.0] * n
+        for j in range(n - 1, -1, -1):
+            way[j] = calls[j][4] + calls[j][5] + max([wk + way[k] for k, wk in succ[j]] + [0.0])
+        free, est, order, avail = {}, [0.0] * n, [], {}
+        for j in range(n):
+            if not npred[j]:
+                avail.setdefault(calls[j][0], []).append(j)
+        while len(order) < n:
+            best = None
+            for q, a in avail.items():
+                if a:
+                    t0 = free.get(q, 0.0)
+                    s = min(max(t0, est[j]) for j in a)
+                    if best is None or s < best[0]:
+                        best = (s, q)
+            s, q = best
+            t0 = free.get(q, 0.0)
+            j = max((j for j in avail[q] if max(t0, est[j]) <= s + SLACK), key=lambda j: (way[j], -j))
+            avail[q].remove(j)
+            free[q] = max(t0, est[j]) + calls[j][4]
+            order.append(j)
+            for k, wk in succ[j]:
+                est[k] = max(est[k], free[q] + calls[j][5] + wk)
+                npred[k] -= 1
+                if not npred[k]:
+                    avail.setdefault(calls[k][0], []).append(k)
+        for j in order:
+            calls[j][1](calls[j][2], calls[j][3])
 
     def col(x):
         return [x] if isinstance(x, tuple) else []
@@ -130,40 +206,50 @@ def rank_program(g, core, T, topo):
     def ap(x):
         return x[0] if isinstance(x, tuple) else x
 
+    def vcost(o, a, k=1.0):
+        if len(a) > 3:
+            return 0.06 + a[3] * 0.0016
+        if len(o) > 3:
+            return 0.06 + o[3] * 0.0035
+        return max(64, wide(a) * k) * 0.00104
+
     def tt(o, a, b, op):
-        E("v", lambda: V.tensor_tensor(out=o[0], in0=a[0], in1=b[0], op=op), [a, b], [o])
+        k = 1.0 if any(x[1][0][0] in PSUM for x in (a, b)) else 2.0
+        E("v", lambda: V.tensor_tensor(out=o[0], in0=a[0], in1=b[0], op=op), [a, b], [o], vcost(o, a, k))
 
     def ts(o, a, s1, op0, s2=None, op1=None):
-        if op1 is None:
-            E("v", lambda: V.tensor_scalar(out=o[0], in0=a[0], scalar1=ap(s1), scalar2=None, op0=op0), [a] + col(s1), [o])
-        else:
-            E("v", lambda: V.tensor_scalar(out=o[0], in0=a[0], scalar1=ap(s1), scalar2=ap(s2), op0=op0, op1=op1),
-              [a] + col(s1) + col(s2), [o])
+        kw = dict(scalar2=None) if op1 is None else dict(scalar2=ap(s2), op1=op1)
+        k = 0.5 if a[1][0][0] in TWO and o[1][0][0] in TWO else 1.0
+        E("v", lambda: V.tensor_scalar(out=o[0], in0=a[0], scalar1=ap(s1), op0=op0, **kw), [a] + col(s1) + col(s2), [o], vcost(o, a, k))
 
     def cp(o, a):
-        E("v", lambda: V.tensor_copy(out=o[0], in_=a[0]), [a], [o])
+        E("v", lambda: V.tensor_copy(out=o[0], in_=a[0]), [a], [o], vcost(o, a))
 
     def fill(o, c):
-        E("v", lambda: V.memset(o[0], c), [], [o])
+        E("v", lambda: V.memset(o[0], c), [], [o], vcost(o, o))
 
     def act(o, a, f=F.Copy, bias=0.0, scale=1.0):
-        E("s", lambda: S.activation(out=o[0], in_=a[0], func=f, bias=ap(bias), scale=ap(scale)), [a] + col(bias) + col(scale), [o])
+        E("s", lambda: S.activation(out=o[0], in_=a[0], func=f, bias=ap(bias), scale=ap(scale)), [a] + col(bias) + col(scale), [o],
+          vcost(o, a))
 
     def mm(o, l, r, start=True, stop=True):
-        E("t", lambda: PE.matmul(out=o[0], lhsT=l[0], rhs=r[0], start=start, stop=stop), [l, r], [o])
+        k = 4 if l[1][0][0] in BUFS[F32] else 1
+        E("t", lambda: PE.matmul(out=o[0], lhsT=l[0], rhs=r[0], start=start, stop=stop), [l, r], [o], max(64, wide(r)) * k * 0.00104)
 
     def tr(o, a):
-        E("t", lambda: PE.transpose(out=o[0], in_=a[0], identity=w("IDB")[0]), [a, w("IDB")], [o])
+        E("t", lambda: PE.transpose(out=o[0], in_=a[0], identity=w("IDB")[0]), [a, w("IDB")], [o], 0.13)
 
     def iota(o, pat, base, cm):
-        E("g", lambda: g.iota(o[0], pattern=pat, base=base, channel_multiplier=cm, allow_small_or_imprecise_dtypes=True), [], [o])
+        E("g", lambda: g.iota(o[0], pattern=pat, base=base, channel_multiplier=cm, allow_small_or_imprecise_dtypes=True), [], [o],
+          0.15 + 0.002 * wide(o))
 
     def aff(o, a, pat, op, base, cm):
         E("g", lambda: g.affine_select(out=o[0], in_=a[0], pattern=pat, compare_op=op, fill=0.0, base=base, channel_multiplier=cm),
-          [a], [o])
+          [a], [o], 0.2 + 0.002 * wide(o))
 
-    dma("d", T["DET"][:, :], T.det[:, :], "ld0", [], [("DET", (1 << 1024) - 1)])
-    dma("s", T["hamt"][:, :], T.ham[:, :], "ld1", [], [("hamt", (1 << 3584) - 1)])
+    ALL = (1 << 1024) - 1
+    dma("d", T["DET"][:, :], T.det[:, :], "ld0", [], [("DET", ALL)])
+    dma("d", T["hamt"][:, :], T.ham[:, :], "ld1", [("DET", ALL)], [("hamt", (1 << 3584) - 1)])
 
     fill(w("ONEB"), 1.0)
     fill(w("ONE"), 1.0)
@@ -177,7 +263,8 @@ def rank_program(g, core, T, topo):
     for t in range(3):
         iota(w("PK", 8 * t, 8 * t + 8), [[128, 8]], 310 * (t + 1), 1)
     aff(w("TRI"), w("ONEB", 0, 128), [[1, 128]], O.is_ge, -1, -1)
-    iota(w("SW"), [[16, 16]], -1024, 0)
+    iota(w("SW"), [[16, 16]], 1024, 0)
+    iota(w("KD"), [[0, 8], [-2048, 17]], 0, 0)
     aff(w("DM"), w("ONE", 0, 136), [[-16, 8], [0, 17]], O.is_ge, 0, 1)
     aff(w("DM"), w("DM"), [[16, 8], [0, 17]], O.is_ge, 15, -1)
     aff(w("IDB"), w("ONEB", 0, 128), [[-1, 128]], O.is_equal, 0, 1)
@@ -194,10 +281,8 @@ def rank_program(g, core, T, topo):
     aff(w("WT", 0, 16), w("WT", 0, 16), [[0, 2], [-16, 8]], O.is_ge, 0, 1)
     aff(w("WT", 0, 16), w("WT", 0, 16), [[0, 2], [16, 8]], O.is_ge, 15, -1)
     aff(w("WT", 16, 24), w("ONE", 0, 8), [[-16, 8]], O.is_equal, -15, 1)
-    ts(w("PL"), w("PK"), 255, O.bitwise_and)
-    ts(w("PA"), w("PL"), 0.5, O.mult)
-    ts(w("PL"), w("PK"), 768, O.bitwise_and)
-    ts(w("PB"), w("PL"), -2048.0, O.add, 0.5, O.mult)
+    ts(w("PL"), w("PK"), 1023, O.bitwise_and)
+    ts(w("PA"), w("PL"), -2048.0, O.add, 0.5, O.mult)
     ts(w("PI"), w("PI"), 15, O.bitwise_and)
     ts(w("MR"), w("PI"), 0.0, O.is_equal)
     ts(w("PJ"), w("PJ"), 15, O.bitwise_and)
@@ -240,14 +325,14 @@ def rank_program(g, core, T, topo):
     fill(w("TD", 1024, 1280), 0.0)
     fill(w("ZG"), 0.0)
     cp(w("ZG", 8, 16), w("G8"))
-    ts(w("G16"), w("G8"), 16.0, O.mult)
+    ts(w("G16"), w("G8"), 16.0 * 37, O.mult)
     SEL = [w("ZG", 8, 24), w("ZG", 0, 16)]
 
     for h in range(2):
         aff(w("SVX%d" % h), w("ONEB", 0, 128), [[-2, 8], [0, 16]], O.is_equal, -16 - h, 1)
     iota(w("TRS"), [[0, 8], [128, 2]], 256, 1)
     iota(w("TRA"), [[0, 8], [128, 2]], 1024, 1)
-    iota(w("MC"), [[1, 10], [0, 16]], 20, 0)
+    iota(w("MC"), [[1, 10], [0, 16]], 2048, 0)
     iota(w("IM"), [[1, 10], [0, 16]], 0, 0)
     iota(w("XI"), [[16, 8]], 0, 0)
     iota(w("XJ"), [[0, 1]], 0, 1)
@@ -286,6 +371,7 @@ def rank_program(g, core, T, topo):
         for c in range(8):
             ts(w("WC", 8 * c, 8 * c + 8), w("G8"), w("WX", c, c + 1), O.mult)
         ts(w("WBIG"), w("G8"), 1e29, O.mult)
+        ts(w("IDN"), w("IDB"), -1 / 256, O.mult)
 
     def t2w(src, n, X):
         for r in range(16):
@@ -299,28 +385,32 @@ def rank_program(g, core, T, topo):
     far = [q for q in peers if q not in near]
 
     def send(t):
-        sb, plan, used = "SB%d" % t, [], []
+        sb, plan, used, share = "SB%d" % t, [], [], []
         for i, q in enumerate(far):
             e = topo.engines(core, T.cores[q])
             k = len(e) // len(far)
+            share.append(k)
             plan.append((q, e[i * k:(i + 1) * k]))
             used += e[i * k:(i + 1) * k]
         for i, q in enumerate(near):
             e = [x for x in topo.engines(core, T.cores[q]) if x not in used]
-            k = len(e) // len(near)
+            k = min([len(e) // len(near)] + share)
             plan.append((q, e[i * k:(i + 1) * k]))
         got = sum(len(e) for q, e in plan)
-        deps("g", w(sb, 0, 256)[1], [])
-        tf = []
-        for q, e in plan:
-            rid, pid = topo.addr(T.cores[q], core)
-            tf.append(RemoteDMATransfer(dst_ids=[DstId(rid=rid, pnc=pid)], dma_engine_mask=sum(1 << x for x in e),
-                                        remote_sem=T.sem["rx%d" % t], src=T[sb][:, 64 * q:64 * q + 64],
-                                        dst=T["IN%d" % t][:, 64 * me:64 * me + 64], alu_op=0))
-        g.remote_dma_fused(tf, local_sem=T.sem["snd"])
         rx = "rx%d" % t
-        semof[rx] = (rx, got)
-        note(rx, 1, [], [r for q in peers for r in w("IN%d" % t, 64 * q, 64 * q + 64)[1]])
+
+        def emit(reads, writes):
+            deps("g", reads, [])
+            tf = []
+            for q, e in plan:
+                rid, pid = topo.addr(T.cores[q], core)
+                tf.append(RemoteDMATransfer(dst_ids=[DstId(rid=rid, pnc=pid)], dma_engine_mask=sum(1 << x for x in e),
+                                            remote_sem=T.sem[rx], src=T[sb][:, 64 * q:64 * q + 64],
+                                            dst=T["IN%d" % t][:, 64 * me:64 * me + 64], alu_op=0))
+            g.remote_dma_fused(tf, local_sem=T.sem["snd"])
+            semof[rx] = (rx, got)
+            note(rx, 1, [], writes)
+        calls.append(("g", emit, w(sb, 0, 256)[1], [r for q in peers for r in w("IN%d" % t, 64 * q, 64 * q + 64)[1]], 0.5, 4.0))
         act(w("IN%d" % t, 64 * me, 64 * me + 64), w(sb, 64 * me, 64 * me + 64))
         return got
 
@@ -335,12 +425,9 @@ def rank_program(g, core, T, topo):
     for t in range(3):
         IN, SB = "IN%d" % t, "SB%d" % t
         if t:
-            for i, (a, b) in enumerate(((0, 256), (256, 512), (512, 768), (768, 1024))):
-                for x, y, p in rot(t, a, b):
-                    if i % 2:
-                        cp(w("QB", x, y), w("QT", p, p + y - x))
-                    else:
-                        act(w("QB", x, y), w("QT", p, p + y - x))
+            for a in range(0, 1024, 256):
+                for x, y, p in rot(t, a, a + 256):
+                    act(w("QB", x, y), w("QT", p, p + y - x))
         for k in range(8):
             mm(w("P0", 8 * k, 8 * k + 8), w("QB", 128 * k, 128 * k + 128), w("SEL8") if t else w("G8"))
         ts(w("LV"), w("P0", 0, 64), 0.0, O.is_gt)
@@ -349,7 +436,7 @@ def rank_program(g, core, T, topo):
         for d in range(1, 8):
             mm(w("P1", 8 * d, 64), w("ONEB", 0, 128), w("LV", 0, 64 - 8 * d), False, d == 7)
         tt(w("RF"), w("P1", 0, 64), w("DB"), O.add)
-        cp(w("R32"), w("RF"))
+        tt(w("R32"), w("P1", 0, 64), w("DB"), O.add)
         ts(w("LOW"), w("R32"), 15, O.bitwise_and)
         for h in range(17):
             act(w("BS", h, 1088, 17), w("RF"), F.Sign, 0.5 - 16 * h)
@@ -360,10 +447,9 @@ def rank_program(g, core, T, topo):
         for k in range(8):
             c = (128 * k, 128 * k + 128)
             ts(w("OA", *c), w("OL", *c), w("PA", 8 * t + k, 8 * t + k + 1), O.mult)
-            act(w("OB", *c), w("OL", *c), F.Copy, 0.0, w("PB", 8 * t + k, 8 * t + k + 1))
+        mm(w("P2", 0, 136), w("C128"), w("KD"), True, False)
         for k in range(8):
-            for i, n in enumerate(("OA", "OB")):
-                mm(w("P2", 0, 136), w(n, 128 * k, 128 * k + 128), w("BS", 136 * k, 136 * k + 136), k + i == 0, k + i == 8)
+            mm(w("P2", 0, 136), w("OA", 128 * k, 128 * k + 128), w("BS", 136 * k, 136 * k + 136), False, k == 7)
         for k in range(8):
             mm(w("P0", 0, 8), w("ONEB", 0, 128), w("LV", 8 * k, 8 * k + 8), k == 0, k == 7)
         if t:
@@ -372,8 +458,7 @@ def rank_program(g, core, T, topo):
         for n in (68, 34, 17):
             tt(w("LM", 0, n), w("LM", 0, n), w("LM", n, 2 * n), O.add)
         tt(w("LD"), w("LM", 0, 16), w("LM", 1, 17), O.subtract)
-        tt(w("LE"), w("LD"), w("SW"), O.min)
-        ts(w("GU"), w("LE"), 2048.0, O.add)
+        tt(w("GU"), w("LD"), w("SW"), O.min)
         act(w("AB"), ind(w("TC"), w("GU")), F.Abs)
         mm(w("P3", 0, 256), w("IDB"), w("AB"))
         cp(w("DU"), ind(w("TD"), w("GU")))
@@ -390,26 +475,30 @@ def rank_program(g, core, T, topo):
             mm(w("P0", 64 + h, 96, 2), w("DF", 128 * h, 128 * h + 128), w("WT", 0, 16))
 
         def mins(a, b):
-            for k in range(16):
+            for k in list(range(8, 16)) + list(range(8)):
                 tt(w("MK", 256 * k + a, 256 * k + b), w("hv", 16 * a + k, 16 * b, 16), w("P3", a, b), O.min)
 
+        UP = ["P1", "P6"]
+
         def tree(h):
-            p = "P%d" % (1 + h)
-            mm(w(p, 0, 128), w("C128"), w("KC"), True, False)
-            for k in range(16):
-                mm(w(p, 8 * k, 8 * k + 8), w("MK", 256 * k + 128 * h, 256 * k + 128 * h + 128), w("G16"), False, k == 15)
+            for p, ks in ((UP[h], range(8, 16)), ("P%d" % (1 + h), range(8))):
+                mm(w(p, 8 * ks[0], 8 * ks[0] + 64), w("C128"), w("KC", 8 * ks[0], 8 * ks[0] + 64), True, False)
+                for k in ks:
+                    mm(w(p, 8 * k, 8 * k + 8), w("MK", 256 * k + 128 * h, 256 * k + 128 * h + 128), w("G16"), False, k == ks[-1])
+            cp(w("EM" if h else "EU"), w(UP[h], 64, 128))
 
         def top(h):
             p, o = "P%d" % (1 + h), 128 * h
-            cp(w("EM"), w(p, 64, 128))
-            tt(w("EA", o, o + 64), w(p, 0, 64), w("EM"), O.max)
+            tt(w("ET", o, o + 64), w(p, 0, 64), w("EM" if h else "EU"), O.max)
             for n in (32, 16):
-                tt(w("EA", o, o + n), w("EA", o, o + n), w("EA", o + n, o + 2 * n), O.max)
-            tt(w("MX", h, 16, 2), w("EA", o, o + 8), w("EA", o + 8, o + 16), O.max)
+                tt(w("ET", o, o + n), w("ET", o, o + n), w("ET", o + n, o + 2 * n), O.max)
+            tt(w("MX", h, 16, 2), w("ET", o, o + 8), w("ET", o + 8, o + 16), O.max)
         mm(w("P4", 0, 256), w("SHP"), w("DF"))
         mm(w("P4", 256, 512), w("SHN"), w("DF"), True, False)
         mm(w("P4", 256, 512), w("BIGL"), w("ONEB"), False, True)
         mm(w("P5", 0, 256), w("NEGI"), w("DF"), True, False)
+        act(w("DP"), w("P4", 0, 256))
+        act(w("DN"), w("P4", 256, 512))
         if t == 0:
             first_qt(0)
         mins(0, CUT[2])
@@ -428,8 +517,7 @@ def rank_program(g, core, T, topo):
         top(1)
         ts(w("F4", 32, 48), w("MX"), 15, O.bitwise_and)
         ts(w("E1"), w("MX"), 4, O.arith_shift_right)
-        ts(w("E2"), w("E1"), 37.0, O.mult)
-        tt(w("E3"), w("E2"), w("HV"), O.add)
+        tt(w("E3"), w("E1"), w("HV"), O.add)
         ts(w("F4", 0, 16), w("E3"), 6, O.arith_shift_right, 63, O.bitwise_and)
         ts(w("F4", 16, 32), w("E3"), 63, O.bitwise_and)
         cp(w("F4B"), w("F4"))
@@ -437,13 +525,13 @@ def rank_program(g, core, T, topo):
         r4 = w("R4", 0, 128, 1, 48)
         cp(r4, w("TP", 0, 128, 1, 48))
         for h in range(2):
-            mm(w("P6", 256 + 128 * h, 384 + 128 * h), w("SK%d" % h, 0, 128, 1, 48), r4)
+            mm(w("P2", 128 * h, 128 * h + 128), w("SK%d" % h, 0, 128, 1, 48), r4)
         for h in range(2):
             mm(w("P6", 128 * h, 128 * h + 128), w("SV%d" % h, 0, 128, 1, 48), r4)
         for h in range(2):
             mm(w("P5", 128 * h, 128 * h + 128), w("SV%d" % h, 0, 128, 1, 48), r4, False, h == 1)
-        act(w("P0", 0, 256), w("P6", 256, 512), F.Relu, w("B2"), 8192.0)
-        act(w("P1", 0, 256), w("P6", 256, 512), F.Relu, w("B1"), -8192.0)
+        act(w("P0", 0, 256), w("P2", 0, 256), F.Relu, w("B2"), 8192.0)
+        act(w("P1", 0, 256), w("P2", 0, 256), F.Relu, w("B1"), -8192.0)
         act(w("SG"), w("P5", 0, 256), F.Sign)
         ts(w("FI"), w("CN"), 0.25, O.mult, -0.375, O.add)
         ts(w("KM2"), w("F4", 32, 48), 2.0, O.mult)
@@ -451,12 +539,12 @@ def rank_program(g, core, T, topo):
         ts(w("VV"), w("E3"), 4095, O.bitwise_and)
         ts(w("OK1"), w("VV"), 3584.0, O.is_lt)
         tt(w("OK1"), w("OK1"), w("ON"), O.mult)
-        tt(w("EA"), w("DF"), w("P0", 0, 256), O.add)
-        tt(w("EB"), w("EA"), w("P6", 0, 256), O.min)
-        tt(w("EC"), w("EB"), w("P4", 256, 512), O.min)
-        tt(w("ED"), w("DF"), w("P1", 0, 256), O.subtract)
-        tt(w("EA"), w("EC"), w("P4", 0, 256), O.max)
-        tt(w("CH"), w("EA"), w("ED"), O.max)
+        tt(w("EB"), w("DN"), w("P6", 0, 256), O.min)
+        tt(w("P0", 0, 256), w("DF"), w("P0", 0, 256), O.add)
+        tt(w("P1", 0, 256), w("DF"), w("P1", 0, 256), O.subtract)
+        tt(w("EC"), w("EB"), w("P0", 0, 256), O.min)
+        tt(w("P1", 0, 256), w("DP"), w("P1", 0, 256), O.max)
+        tt(w("CH"), w("EC"), w("P1", 0, 256), O.max)
         for h in range(2):
             mm(w("P3", h, 16, 2), w("SG", 128 * h, 128 * h + 128), w("G8"))
         for h in range(2):
@@ -465,11 +553,11 @@ def rank_program(g, core, T, topo):
         cp(w("SGI"), w("P3", 0, 16))
         tt(w("N1"), w("SGI"), w("KM2"), O.add)
         ts(w("N2"), w("N1"), 14.0, O.is_gt)
-        ts(w("N1"), w("SGI"), 1, O.arith_shift_right)
-        tt(w("N3"), w("N1"), w("N2"), O.add)
-        tt(w("N2"), w("N3"), w("KM1"), O.add)
-        ts(w("N1"), w("N2"), 1, O.bitwise_and)
-        ts(w("SNB"), w("N1"), -2.0, O.mult, 1.0, O.add)
+        ts(w("N4"), w("SGI"), 1, O.arith_shift_right)
+        tt(w("N5"), w("N4"), w("KM1"), O.add)
+        tt(w("N6"), w("N5"), w("N2"), O.add)
+        ts(w("N7"), w("N6"), 1, O.bitwise_and)
+        ts(w("SNB"), w("N7"), -2.0, O.mult, 1.0, O.add)
         tr(w("TP", 0, 128, 1, 16), w("SNB"))
         ts(w("N3"), w("SGI"), 1, O.bitwise_and)
         ts(w("SN0"), w("N3"), 0.0, O.is_equal)
@@ -494,10 +582,10 @@ def rank_program(g, core, T, topo):
         tt(w("K4"), w("K2", 0, 16), w("K2", 16, 32), O.add)
         ts(w("K5"), w("K4"), 64.0, O.is_ge, 1024.0, O.mult)
         ts(w("K6"), w("K3"), 64.0, O.mult)
-        tt(w("K6"), w("K6"), w("K4"), O.add)
-        tt(w("K5"), w("K5"), w("K6"), O.add)
+        tt(w("K7"), w("K6"), w("K4"), O.add)
+        tt(w("K8"), w("K5"), w("K7"), O.add)
         for h in range(2):
-            tt(w("FS", 8 * h, 8 * h + 8), w("K5", h, 16, 2), w("TRS", h, 16, 2), O.min)
+            tt(w("FS", 8 * h, 8 * h + 8), w("K8", h, 16, 2), w("TRS", h, 16, 2), O.min)
         t2w(w("FS"), 16, "XF")
         for h in range(2):
             mm(w("P6", 0, 16), w("XF", 128 * h, 128 * h + 128), SEL[h], h == 0, h == 1)
@@ -519,8 +607,9 @@ def rank_program(g, core, T, topo):
         cp(ind(w("QT"), w("GU")), w("QS"))
         if t == 2:
             for b in range(2):
-                act(w("P5", 0, 512), w("TD", 512 * b, 512 * b + 512), F.Copy, 128.0, 256.0)
-                tt(w("YT", 512 * b, 512 * b + 512), w("P5", 0, 512), w("TC", 512 * b, 512 * b + 512), O.add)
+                mm(w("P5", 0, 512), w("NEGI"), w("TD", 512 * b, 512 * b + 512), True, False)
+                mm(w("P5", 0, 512), w("IDN"), w("TC", 512 * b, 512 * b + 512), False, True)
+                act(w("YT", 512 * b, 512 * b + 512), w("P5", 0, 512), F.Copy, 128.0, -256.0)
         ts(w("AT", 0, 128), w(IN, 0, 128), 1 / 256, O.mult, MAG, O.add)
         act(w("AT", 128, 256), w(IN, 128, 256), F.Identity, MAG, 1 / 256)
         ts(w("AD", 0, 128), w("AT", 0, 128), -MAG, O.add)
@@ -542,8 +631,9 @@ def rank_program(g, core, T, topo):
         t2w(w("ZF"), 64, "XB")
         act(w("QA"), w("P2", 0, 256))
         ts(w("HQ"), w("JP"), 7, O.arith_shift_right, 1023, O.bitwise_and)
-        ts(w("ST"), w("J2", 0, 16), 2.0, O.mult, 1.0, O.add)
-        ts(w("NU"), w("J1", 32, 48), 1.0, O.is_lt, 40.0, O.mult)
+        ts(w("ST0"), w("J2", 0, 16), 511, O.bitwise_and)
+        ts(w("ST"), w("ST0"), 2.0, O.mult, 1.0, O.add)
+        ts(w("NU"), w("J1", 32, 48), 1.0, O.is_lt, 4096.0, O.mult)
         tt(w("P6", 0, 256), w(IN), w("P6", 0, 256), O.add)
         for c in range(2):
             for h in range(2):
@@ -557,22 +647,22 @@ def rank_program(g, core, T, topo):
 
         def probe(m):
             o = w("CMP", 256 * m, 256 * m + 256)
-            if m < 5:
+            if m < 4:
                 tt(o, ind(w("QT", 0, 1024), w("ZU", 16 * m, 16 * m + 16)), w("QA"), O.is_equal)
             else:
-                tt(o, w("PR5", 256 * (m - 5), 256 * (m - 4)), w("P2", 0, 256), O.is_equal)
+                tt(o, w("PR5", 256 * (m - 4), 256 * (m - 3)), w("P2", 0, 256), O.is_equal)
             for h in range(2):
                 mm(w("P%d" % (5 if m < 5 else 0), 16 * (m % 5) + h, 16 * (m % 5) + 16, 2),
                    w("CMP", 256 * m + 128 * h, 256 * m + 128 * h + 128), w("RW"))
 
         def score(c):
             p, z = w("P%d" % (0 if c else 5), 0, 80), (80 * c, 80 * c + 80)
-            ts(w("S1", *z), p, 8.0, O.is_equal, -10.0, O.mult)
-            ts(w("S2", *z), p, 8.0, O.is_ge, -10.0, O.mult)
-            tt(w("S3", *z), w("S1", *z), w("S2", *z), O.add)
-            tt(w("S1", *z), w("S3", *z), w("MC", *z), O.add)
-        for m in range(5):
-            act(w("PR5", 256 * m, 256 * m + 256), ind(w("QT", 0, 1024), w("ZU", 16 * m + 80, 16 * m + 96)))
+            ts(w("S2", *z), p, 8.0, O.is_ge, -1024.0, O.mult)
+            ts(p, p, 8.0, O.is_equal, -1024.0, O.mult)
+            tt(w("S3", *z), w("S2", *z), w("MC", *z), O.add)
+            tt(w("S1", *z), p, w("S3", *z), O.add)
+        for m in range(6):
+            act(w("PR5", 256 * m, 256 * m + 256), ind(w("QT", 0, 1024), w("ZU", 16 * m + 64, 16 * m + 80)))
         for m in range(6):
             probe(m)
         score(0)
@@ -583,17 +673,17 @@ def rank_program(g, core, T, topo):
         tt(w("S5"), w("S4", 0, 32), w("S4", 32, 64), O.min)
         tt(w("S6"), w("S5", 0, 16), w("S5", 16, 32), O.min)
         tt(w("S7"), w("S6"), w("S4", 64, 80), O.min)
-        ts(w("M1"), w("S7"), 10.0, O.is_ge, -10.0, O.mult)
-        tt(w("M2"), w("M1"), w("S7"), O.add)
-        tt(w("M3"), w("M2"), w("ST"), O.mult)
-        tt(w("S6"), w("S7"), w("NU"), O.add)
-        ts(w("M4"), w("S6"), 20.0, O.is_ge, 2048.0, O.mult)
-        tt(w("N1"), w("M3"), w("HQ"), O.add)
-        ts(w("N2"), w("N1"), 1023, O.bitwise_and)
-        tt(w("PLC"), w("N2"), w("M4"), O.add)
-        ts(w("DG", 0, 16), w("PLC"), 6, O.arith_shift_right)
-        ts(w("DG", 16, 32), w("PLC"), 63, O.bitwise_and)
-        cp(w("FD"), w("DG"))
+        tt(w("M3"), w("S7"), w("ST"), O.mult)
+        tt(w("SN"), w("S7"), w("NU"), O.add)
+        ts(w("M4"), w("SN"), 2048.0, O.is_ge, 2048.0, O.mult)
+        ts(w("M5"), w("SN"), 2048.0, O.is_ge, 32.0, O.mult)
+        tt(w("PN"), w("M3"), w("HQ"), O.add)
+        ts(w("DG", 0, 16), w("PN"), 6, O.arith_shift_right, 15, O.bitwise_and)
+        ts(w("DG", 16, 32), w("PN"), 63, O.bitwise_and)
+        tt(w("FD", 0, 16), w("DG", 0, 16), w("M5"), O.add)
+        cp(w("FD", 16, 32), w("DG", 16, 32))
+        ts(w("PM"), w("PN"), 1023, O.bitwise_and)
+        tt(w("PLC"), w("PM"), w("M4"), O.add)
         tr(w("TP", 0, 128, 1, 32), w("FD"))
         for h in range(2):
             cp(w("PF", 8 * h, 8 * h + 8), w("PLC", h, 16, 2))
@@ -605,6 +695,18 @@ def rank_program(g, core, T, topo):
             mm(w("P1", 0, 16), w("XF", 128 * h, 128 * h + 128), SEL[h], h == 0, h == 1)
         cp(w("PU"), w("P0", 0, 256))
         cp(w("PW"), w("P1", 0, 16))
+        ts(w("PO"), w("PW"), 1279.0, O.min)
+        act(w("CO"), ind(w("TC"), w("PO")))
+        if t == 2:
+            act(w("P1", 0, 256), w("AD"), F.Copy, 128.0, 256.0)
+        tt(w("CV"), w("CO"), w("P6", 0, 256), O.add)
+        ts(w("CNW"), w("CV"), 127.0, O.min, -127.0, O.max)
+        if t < 2:
+            act(w("ABN"), w("CNW"), F.Abs)
+            mm(w("P2", 0, 256), w("R8"), w("ABN"))
+            tt(w("QN"), w("QA"), w("P2", 0, 256), O.add)
+        else:
+            tt(w("YN"), w("CNW"), w("P1", 0, 256), O.add)
         for c in range(16):
             a = 0 if c < 8 else 128
             ts(w("MK", 256 * c + a, 256 * c + 256), w("PU", a, 256), w("PW", c, c + 1), O.is_equal)
@@ -621,21 +723,13 @@ def rank_program(g, core, T, topo):
         for h in range(2):
             mm(w("P5", 0, 16), w("XF", 128 * h, 128 * h + 128), SEL[h], h == 0, h == 1)
         cp(w("FO"), w("P5", 0, 16))
-        act(w("CO"), ind(w("TC"), w("FO")))
-        if t == 2:
-            act(w("P1", 0, 256), w("AD"), F.Copy, 128.0, 256.0)
-        tt(w("EB"), w("CO"), w("P6", 0, 256), O.add)
-        ts(w("CNW"), w("EB"), 127.0, O.min, -127.0, O.max)
         if t < 2:
-            act(w("ABF"), w("CNW"), F.Abs)
-            mm(w("P2", 0, 256), w("R8"), w("ABF"))
+            cp(ind(w("QT"), w("FO")), w("QN"))
             cp(ind(w("TC"), w("FO")), w("CNW"))
-            tt(w("QS"), w("QA"), w("P2", 0, 256), O.add)
-            cp(ind(w("QT"), w("FO")), w("QS"))
         else:
-            tt(w("YN"), w("CNW"), w("P1", 0, 256), O.add)
             cp(ind(w("YT"), w("FO")), w("YN"))
             dma("d", T.y[:, :], T["YT"][:, 0:1024], "st0", w("YT", 0, 1024)[1], [])
+    schedule()
     wait("d", "st0", 1)
     g.wait_ge(T.sem.snd, sent)
     for q in ("v", "s", "t", "g"):

@@ -2,21 +2,21 @@ from concourse.bass import DstId, RemoteDMATransfer
 from concourse.mybir import AluOpType as O, ActivationFunctionType as F
 import math
 
-WAKE, SLACK = 0.10, 0.05
+WAKE, SLACK, BETA = 0.15, 0.03, 1.2
 F32, BF, I32, U16, F16 = "float32", "bfloat16", "int32", "uint16", "float16"
 BUFS = {
     F32: dict(TD=1280, QT=1280, ONE=160, NEGI=128, ZG=24, WT=24, SHP=128, SHN=128, QW=128, QE=128, DM=136, SW=16, SC=2, TRS=16,
               TRA=16, WX=8, XI=8, THR=1, XJ=1, RC=1, B1=1, B2=1, MC=160, MR=16, PA=24, TV=1024, TM=1024, DB=64, RF=64,
               LM=136, LD=16, DF=256, EM=64, EU=64, ET=256, EB=256, EC=256, ED=256, DP=256, DN=256, CH=256, CF32=256, ON=16,
-              OK1=16, SN0=16, K1=64, K2=32, K3=16, K4=16, K5=16, K6=16, K7=16, K8=16, FS=16, XF=256, AT=256, AD=256, QA=256,
-              QS=256, QN=256, CV=256, ZF=64, ST=16, S1=160, S2=160, S3=160, S4=80, S5=32, S6=16, S7=16, SN=16, M1=16, M3=16,
-              M4=16, M5=16, NU=16, PW=16, LO=16, YT=1280, YN=256, PR5=1536, BAD=16, SB0=512, SB1=512, SB2=512, IN0=256,
+              OK1=16, SN0=16, QQ=64, K1=64, K2=32, K5=64, K6=64, K7=64, K8=16, FS=16, XF=256, AT=256, AD=256, QA=256,
+              QS=256, QN=256, CV=256, ZF=64, ST=16, S1=160, S2=160, S3=160, S4=80, S5=32, S6=16, S7=16, SN=16, PT=16, M3=16,
+              M4=16, M5=16, NU=16, PW=16, LO=16, YT=1280, YN=256, PR5=1536, SB0=512, SB1=512, SB2=512, IN0=256,
               IN1=256, IN2=256, PF=32),
     BF: dict(TC=1280, ham=3584, ONEB=256, G8=8, G16=8, SEL8=8, SELB=8, RW=8, TRI=128, IDB=128, IDN=128, KC=128, KD=136, C128=128,
              C64=128, BIGL=128, R8=128, WC=128, WBIG=8, ZW=1280, IM=160, SV0=128, SV1=128, SK0=128, SK1=128, SS0=128, SS1=128,
              QB=1024, LV=64, OL=1024, BS=1088, AB=256, CN=256, hv=4096, MK=4096, F4B=48, R4=128, SG=256, SNB=16, R5=128, OM=64,
              CFD=256, ABF=256, ABN=256, XB=1024, CMP=2560, FD=32, R6=128, CO=256, CNW=256, SVX0=128, SVX1=128),
-    I32: dict(DET=1024, CI=1024, PI=16, PJ=1, PK=24, PL=24, R32=64, LOW=64, MX=16, E1=16, E3=16, VV=16, F4=48, H1=32,
+    I32: dict(DET=1024, CI=1024, PI=16, PJ=1, PK=24, PL=24, R32=64, LOW=64, MX=16, E3=16, VV=16, F4=48, H1=32,
               H2=32, HP=16, HV=16, SGI=16, N1=16, N2=16, N3=16, N4=16, N5=16, N6=16, N7=16, KM2=16, KM1=16, FI=256, I1=32, I2=32,
               PR=16, OW=16, J1=48, J2=32, JP=16, ZD=64, ZI=160, ZJ=160, HQ=16, ST0=16, PN=16, PM=16, PLC=16, DG=32, SL2=16),
     F16: dict(OA=1024),
@@ -125,9 +125,6 @@ def rank_program(g, core, T, topo):
             f().then_inc(T.sem[semof[q][0]], 1)
             note(q, cnt[q], reads, writes)
         reads = [r for x in ins for r in x[1] + x[2]] + [r for x in outs for r in x[2]]
-        for x in ins + outs:
-            if len(x) > 3:
-                reads = reads + x[2]
         calls.append((q, emit, reads, [r for x in outs for r in x[1]], cost, 0.0))
 
     def dma(q, out, in_, sem, reads, writes):
@@ -189,6 +186,11 @@ def rank_program(g, core, T, topo):
             s, q = best
             t0 = free.get(q, 0.0)
             j = max((j for j in avail[q] if max(t0, est[j]) <= s + SLACK), key=lambda j: (way[j], -j))
+            soon = [i for i in avail[q] if way[i] > way[j] and s + SLACK < est[i] < s + calls[j][4] - BETA * (est[i] - s)]
+            if soon:
+                i = max(soon, key=lambda i: way[i])
+                fit = [f for f in avail[q] if max(t0, est[f]) + calls[f][4] <= est[i] + SLACK]
+                j = max(fit, key=lambda f: (way[f], -f)) if fit else i
             avail[q].remove(j)
             free[q] = max(t0, est[j]) + calls[j][4]
             order.append(j)
@@ -510,16 +512,15 @@ def rank_program(g, core, T, topo):
         ts(w("H2"), w("H1"), 4095, O.bitwise_and)
         tt(w("HP"), w("H2", 0, 16), w("H2", 16, 32), O.mult)
         ts(w("HP"), w("HP"), 5, O.arith_shift_right)
-        ts(w("HV"), w("HP"), float(t), O.add)
+        ts(w("HV"), w("HP"), 16.0, O.mult, 16.0 * t, O.add)
         top(0)
         mins(CUT[3], CUT[4])
         tree(1)
         top(1)
         ts(w("F4", 32, 48), w("MX"), 15, O.bitwise_and)
-        ts(w("E1"), w("MX"), 4, O.arith_shift_right)
-        tt(w("E3"), w("E1"), w("HV"), O.add)
-        ts(w("F4", 0, 16), w("E3"), 6, O.arith_shift_right, 63, O.bitwise_and)
-        ts(w("F4", 16, 32), w("E3"), 63, O.bitwise_and)
+        tt(w("E3"), w("MX"), w("HV"), O.add)
+        ts(w("F4", 0, 16), w("E3"), 10, O.arith_shift_right, 63, O.bitwise_and)
+        ts(w("F4", 16, 32), w("E3"), 4, O.arith_shift_right, 63, O.bitwise_and)
         cp(w("F4B"), w("F4"))
         tr(w("TP", 0, 128, 1, 48), w("F4B"))
         r4 = w("R4", 0, 128, 1, 48)
@@ -536,7 +537,7 @@ def rank_program(g, core, T, topo):
         ts(w("FI"), w("CN"), 0.25, O.mult, -0.375, O.add)
         ts(w("KM2"), w("F4", 32, 48), 2.0, O.mult)
         ts(w("KM1"), w("F4", 32, 48), 1.0, O.add)
-        ts(w("VV"), w("E3"), 4095, O.bitwise_and)
+        ts(w("VV"), w("E3"), 4, O.arith_shift_right, 4095, O.bitwise_and)
         ts(w("OK1"), w("VV"), 3584.0, O.is_lt)
         tt(w("OK1"), w("OK1"), w("ON"), O.mult)
         tt(w("EB"), w("DN"), w("P6", 0, 256), O.min)
@@ -562,7 +563,8 @@ def rank_program(g, core, T, topo):
         ts(w("N3"), w("SGI"), 1, O.bitwise_and)
         ts(w("SN0"), w("N3"), 0.0, O.is_equal)
         tt(w("OK1"), w("OK1"), w("SN0"), O.mult)
-        ts(w("BAD"), w("OK1"), -8.0, O.mult, 8.0, O.add)
+        for q in range(4):
+            ts(w("QQ", 16 * q, 16 * q + 16), w("OK1"), -8.0, O.mult, 8.0 + q, O.add)
         cp(w("R5", 0, 128, 1, 16), w("TP", 0, 128, 1, 16))
         for h in range(2):
             mm(w("P0", 128 * h, 128 * h + 128), w("SS%d" % h, 0, 128, 1, 16), w("R5", 0, 128, 1, 16))
@@ -570,20 +572,19 @@ def rank_program(g, core, T, topo):
         ts(w("I2"), w("I1"), 4095, O.bitwise_and)
         tt(w("PR"), w("I2", 0, 16), w("I2", 16, 32), O.mult)
         ts(w("OW"), w("PR"), 5, O.arith_shift_right, 3, O.bitwise_and)
-        tt(w("K3"), w("OW"), w("BAD"), O.add)
         for q in range(4):
-            ts(w("OM", 16 * q, 16 * q + 16), w("K3"), float(q), O.is_equal)
+            tt(w("OM", 16 * q, 16 * q + 16), w("OW"), w("QQ", 16 * q, 16 * q + 16), O.is_equal)
         mm(w("P5", 0, 64), w("TRI"), w("OM"), True, False)
         for q in range(4):
             mm(w("P5", 16 * q + 1, 16 * q + 16, 2), w("ONEB", 0, 128), w("OM", 16 * q, 16 * q + 16, 2), False, q == 3)
         tt(w("CF32"), w("FI"), w("P0", 0, 256), O.mult)
-        tt(w("K1"), w("P5", 0, 64), w("OM"), O.mult)
-        tt(w("K2"), w("K1", 0, 32), w("K1", 32, 64), O.add)
-        tt(w("K4"), w("K2", 0, 16), w("K2", 16, 32), O.add)
-        ts(w("K5"), w("K4"), 64.0, O.is_ge, 1024.0, O.mult)
-        ts(w("K6"), w("K3"), 64.0, O.mult)
-        tt(w("K7"), w("K6"), w("K4"), O.add)
-        tt(w("K8"), w("K5"), w("K7"), O.add)
+        for q in range(4):
+            ts(w("K1", 16 * q, 16 * q + 16), w("OM", 16 * q, 16 * q + 16), -4096.0, O.mult, 4096.0 + 64 * q, O.add)
+        ts(w("K5"), w("P5", 0, 64), 64.0, O.is_ge, 4096.0, O.mult)
+        tt(w("K6"), w("P5", 0, 64), w("K1"), O.add)
+        tt(w("K7"), w("K5"), w("K6"), O.add)
+        tt(w("K2"), w("K7", 0, 32), w("K7", 32, 64), O.min)
+        tt(w("K8"), w("K2", 0, 16), w("K2", 16, 32), O.min)
         for h in range(2):
             tt(w("FS", 8 * h, 8 * h + 8), w("K8", h, 16, 2), w("TRS", h, 16, 2), O.min)
         t2w(w("FS"), 16, "XF")
@@ -644,6 +645,7 @@ def rank_program(g, core, T, topo):
             cp(w("ZI", *z), w("P%d" % (3 + c), 0, 80))
             ts(w("ZJ", *z), w("ZI", *z), 1023, O.bitwise_and)
             cp(w("ZU", *z), w("ZJ", *z))
+        SCP = ["P5", "P0", "P1"]
 
         def probe(m):
             o = w("CMP", 256 * m, 256 * m + 256)
@@ -652,11 +654,12 @@ def rank_program(g, core, T, topo):
             else:
                 tt(o, w("PR5", 256 * (m - 4), 256 * (m - 3)), w("P2", 0, 256), O.is_equal)
             for h in range(2):
-                mm(w("P%d" % (5 if m < 5 else 0), 16 * (m % 5) + h, 16 * (m % 5) + 16, 2),
+                mm(w(SCP[0 if m < 5 else 1 if m < 8 else 2], 16 * (m % 5) + h, 16 * (m % 5) + 16, 2),
                    w("CMP", 256 * m + 128 * h, 256 * m + 128 * h + 128), w("RW"))
 
         def score(c):
-            p, z = w("P%d" % (0 if c else 5), 0, 80), (80 * c, 80 * c + 80)
+            a, b = ((0, 5), (5, 8), (8, 10))[c]
+            p, z = w(SCP[c], 16 * (a % 5), 16 * (b - 1) % 80 + 16), (16 * a, 16 * b)
             ts(w("S2", *z), p, 8.0, O.is_ge, -1024.0, O.mult)
             ts(p, p, 8.0, O.is_equal, -1024.0, O.mult)
             tt(w("S3", *z), w("S2", *z), w("MC", *z), O.add)
@@ -666,13 +669,20 @@ def rank_program(g, core, T, topo):
         for m in range(6):
             probe(m)
         score(0)
-        for m in range(6, 10):
+        tt(w("S4", 0, 32), w("S1", 0, 32), w("S1", 32, 64), O.min)
+        tt(w("S5", 0, 16), w("S4", 0, 16), w("S4", 16, 32), O.min)
+        tt(w("S6"), w("S5", 0, 16), w("S1", 64, 80), O.min)
+        for m in (6, 7):
             probe(m)
         score(1)
-        tt(w("S4"), w("S1", 0, 80), w("S1", 80, 160), O.min)
-        tt(w("S5"), w("S4", 0, 32), w("S4", 32, 64), O.min)
-        tt(w("S6"), w("S5", 0, 16), w("S5", 16, 32), O.min)
-        tt(w("S7"), w("S6"), w("S4", 64, 80), O.min)
+        tt(w("S4", 32, 48), w("S1", 80, 96), w("S1", 96, 112), O.min)
+        tt(w("S5", 16, 32), w("S4", 32, 48), w("S1", 112, 128), O.min)
+        tt(w("S4", 48, 64), w("S5", 16, 32), w("S6"), O.min)
+        for m in (8, 9):
+            probe(m)
+        score(2)
+        tt(w("S4", 64, 80), w("S1", 128, 144), w("S1", 144, 160), O.min)
+        tt(w("S7"), w("S4", 64, 80), w("S4", 48, 64), O.min)
         tt(w("M3"), w("S7"), w("ST"), O.mult)
         tt(w("SN"), w("S7"), w("NU"), O.add)
         ts(w("M4"), w("SN"), 2048.0, O.is_ge, 2048.0, O.mult)
@@ -684,6 +694,7 @@ def rank_program(g, core, T, topo):
         cp(w("FD", 16, 32), w("DG", 16, 32))
         ts(w("PM"), w("PN"), 1023, O.bitwise_and)
         tt(w("PLC"), w("PM"), w("M4"), O.add)
+        tt(w("PT"), w("PLC"), w("TRA"), O.min)
         tr(w("TP", 0, 128, 1, 32), w("FD"))
         for h in range(2):
             cp(w("PF", 8 * h, 8 * h + 8), w("PLC", h, 16, 2))
@@ -715,10 +726,9 @@ def rank_program(g, core, T, topo):
                 mm(w("P3", 0, 16, 2), w("MK", 256 * c, 256 * c + 128), wc, c == 0, c == 7)
             mm(w("P4", 1, 16, 2), w("MK", 256 * c + 128, 256 * c + 256), wc if c > 7 else w("WBIG"), c == 0, c == 15)
         for h in range(2):
-            ts(w("LO", h, 16, 2), w("P%d" % (3 + h), h, 16, 2), w("THR"), O.is_ge, 4096.0, O.mult)
-        tt(w("M1"), w("LO"), w("PLC"), O.add)
+            ts(w("LO", h, 16, 2), w("P%d" % (3 + h), h, 16, 2), w("THR"), O.is_ge, w("TRA", h, h + 1), O.mult)
         for h in range(2):
-            tt(w("PF", 16 + 8 * h, 24 + 8 * h), w("M1", h, 16, 2), w("TRA", h, 16, 2), O.min)
+            tt(w("PF", 16 + 8 * h, 24 + 8 * h), w("LO", h, 16, 2), w("PT", h, 16, 2), O.max)
         t2w(w("PF", 16, 32), 16, "XF")
         for h in range(2):
             mm(w("P5", 0, 16), w("XF", 128 * h, 128 * h + 128), SEL[h], h == 0, h == 1)

from concourse.bass import DstId, RemoteDMATransfer
from concourse.mybir import AluOpType as O, ActivationFunctionType as F
import math

WAKE, SLACK, BETA = 0.15, 0.03, 1.2
F32, BF, I32, U16, F16 = "float32", "bfloat16", "int32", "uint16", "float16"
BUFS = {
    F32: dict(TD=1280, QT=1280, ONE=160, NEGI=128, ZG=24, WT=24, SHP=128, SHN=128, QW=128, QE=128, DM=136, SW=16, SC=2, TRS=16,
              TRA=16, WX=8, XI=8, THR=1, XJ=1, RC=1, B1=1, B2=1, MC=160, MR=16, PA=24, TV=1024, TM=1024, DB=64, RF=64,
              LM=136, LD=16, DF=256, EM=64, EU=64, ET=256, EB=256, EC=256, ED=256, DP=256, DN=256, CH=256, CF32=256, ON=16,
              OK1=16, SN0=16, QQ=64, K1=64, K2=32, K5=64, K6=64, K7=64, K8=16, FS=16, XF=256, AT=256, AD=256, QA=256,
              QS=256, QN=256, CV=256, ZF=64, ST=16, S1=160, S2=160, S3=160, S4=80, S5=32, S6=16, S7=16, SN=16, PT=16, M3=16,
              M4=16, M5=16, NU=16, PW=16, LO=16, YT=1280, YN=256, PR5=1536, SB0=512, SB1=512, SB2=512, IN0=256,
              IN1=256, IN2=256, PF=32),
    BF: dict(TC=1280, ham=3584, ONEB=256, G8=8, G16=8, SEL8=8, SELB=8, RW=8, TRI=128, IDB=128, IDN=128, KC=128, KD=136, C128=128,
             C64=128, BIGL=128, R8=128, WC=128, WBIG=8, ZW=1280, IM=160, SV0=128, SV1=128, SK0=128, SK1=128, SS0=128, SS1=128,
             QB=1024, LV=64, OL=1024, BS=1088, AB=256, CN=256, hv=4096, MK=4096, F4B=48, R4=128, SG=256, SNB=16, R5=128, OM=64,
             CFD=256, ABF=256, ABN=256, XB=1024, CMP=2560, FD=32, R6=128, CO=256, CNW=256, SVX0=128, SVX1=128),
    I32: dict(DET=1024, CI=1024, PI=16, PJ=1, PK=24, PL=24, R32=64, LOW=64, MX=16, E3=16, VV=16, F4=48, H1=32,
              H2=32, HP=16, HV=16, SGI=16, N1=16, N2=16, N3=16, N4=16, N5=16, N6=16, N7=16, KM2=16, KM1=16, FI=256, I1=32, I2=32,
              PR=16, OW=16, J1=48, J2=32, JP=16, ZD=64, ZI=160, ZJ=160, HQ=16, ST0=16, PN=16, PM=16, PLC=16, DG=32, SL2=16),
    F16: dict(OA=1024),
    U16: dict(GU=16, DU=256, OFF=16, ZU=160, PU=256, PO=16, FO=16),
}
SCRATCH, WIDTH, WHERE = {}, {}, {}
for _d in BUFS:
    _p = 0
    for _n, _w in BUFS[_d].items():
        _n = "hamt" if _n == "ham" else _n
        WIDTH[_n] = _w
        if _w <= 160:
            WHERE[_n] = ("small_" + _d, _p)
            _p += (_w + 15) // 16 * 16
        else:
            SCRATCH[_n] = ("sbuf", [128, _w], _d)
    if _p:
        SCRATCH["small_" + _d] = ("sbuf", [128, _p], _d)
TWO = list(BUFS[F16]) + list(BUFS[BF]) + list(BUFS[U16])
PSUM = ["P%d" % _k for _k in range(7)] + ["TP"]
for _n in PSUM:
    WIDTH[_n] = 128 if _n == "TP" else 512
    SCRATCH[_n] = ("psum", [128, WIDTH[_n]], BF if _n == "TP" else F32)
SEMAPHORES = ["qv", "qs", "qt", "qg", "ld0", "ld1", "st0", "snd", "rx0", "rx1", "rx2"]


def rank_program(g, core, T, topo):
    me = T.rank_of(core)
    if me is None:
        return
    V, S, PE = g.vector, g.scalar, g.tensor
    ENG = {"v": V, "s": S, "t": PE, "g": g, "d": g.sync}
    cnt, known, clk = {"v": 0, "s": 0, "t": 0, "g": 0}, {q: {} for q in ENG}, {}
    wr, rd, last = {}, {}, {}
    semof = {"v": ("qv", 1), "s": ("qs", 1), "t": ("qt", 1), "g": ("qg", 1)}

    def w(name, a=0, b=None, st=1, p=128):
        b = WIDTH[name] if b is None else b
        n, o = WHERE.get(name, (name, 0))
        ap = T[n][0:p, o + a:o + b] if st == 1 else T[n][0:p, o + a:o + b:st]
        m = 0
        if st == 1:
            m = ((1 << (b - a)) - 1) << a
        else:
            for c in range(a, b, st):
                m |= 1 << c
        return (ap, [(name, m)], [])

    def ind(win, off):
        return (win[0].indirect(off[0]), win[1], off[1], 16 * off[1][0][1].bit_count())

    def wait(q, q2, k):
        if known[q].get(q2, 0) >= k:
            return
        sem, inc = semof[q2]
        ENG[q].wait_ge(T.sem[sem], k * inc)
        for a, n in list(clk.get((q2, k), {}).items()) + [(q2, k)]:
            if known[q].get(a, 0) < n:
                known[q][a] = n

    def deps(q, reads, writes):
        need = {}

        def add(q2, k):
            if need.get(q2, 0) < k:
                need[q2] = k
        for n, m in reads + writes:
            if n in PSUM:
                for q2, k in last.get(n, {}).items():
                    if q2 != q:
                        add(q2, k)
        for n, m in reads:
            for q2, k, m2 in wr.get(n, []):
                if m & m2:
                    add(q2, k)
        for n, m in writes:
            for q2, k, m2 in wr.get(n, []):
                if m & m2 and not (q == "t" and q2 == "t"):
                    add(q2, k)
            for q2, k, m2 in rd.get(n, []):
                if m & m2:
                    add(q2, k)
        for q2, k in sorted(need.items(), key=lambda x: x[0] == q):
            wait(q, q2, k)

    def note(q, k, reads, writes):
        clk[(q, k)] = dict(known[q] if q in known else {})
        for n, m in writes:
            wr[n] = [x for x in wr.get(n, []) if x[2] & ~m] + [(q, k, m)]
            rd[n] = [x for x in rd.get(n, []) if x[2] & ~m]
        for n, m in reads:
            rd[n] = [x for x in rd.get(n, []) if not (x[0] == q and not x[2] & ~m)] + [(q, k, m)]
        for n, m in reads + writes:
            if n in PSUM:
                last.setdefault(n, {})[q] = k

    calls = []

    def wide(x):
        return x[3] if len(x) > 3 else x[1][0][1].bit_count()

    def E(q, f, ins, outs, cost):
        def emit(reads, writes):
            deps(q, reads, writes)
            cnt[q] += 1
            f().then_inc(T.sem[semof[q][0]], 1)
            note(q, cnt[q], reads, writes)
        reads = [r for x in ins for r in x[1] + x[2]] + [r for x in outs for r in x[2]]
        calls.append((q, emit, reads, [r for x in outs for r in x[1]], cost, 0.0))

    def dma(q, out, in_, sem, reads, writes):
        def emit(reads, writes):
            deps(q, reads, writes)
            ENG[q].dma_start(out=out, in_=in_).then_inc(T.sem[sem], 16)
            semof[sem] = (sem, 16)
            clk[(sem, 1)] = dict(known[q])
            note(sem, 1, reads, writes)
        calls.append((q, emit, reads, writes, 0.1, 5.0))

    def schedule():
        n = len(calls)
        succ, npred = [[] for _ in range(n)], [0] * n
        W, R, B = {}, {}, {}
        for j, (q, emit, reads, writes, cost, lat) in enumerate(calls):
            pred = {}

            def edge(i, wk):
                pred[i] = max(pred.get(i, 0.0), wk)
            for nm, m in reads + writes:
                if nm in PSUM:
                    for q2, i in B.get(nm, {}).items():
                        edge(i, 0.0 if q2 == q else WAKE)
            for nm, m in reads:
                for i, m2 in W.get(nm, []):
                    if m & m2:
                        edge(i, WAKE)
            for nm, m in writes:
                for i, m2 in W.get(nm, []) + R.get(nm, []):
                    if m & m2:
                        edge(i, 0.0 if q == calls[i][0] == "t" else WAKE)
            for i, wk in pred.items():
                succ[i].append((j, wk))
            npred[j] = len(pred)
            for nm, m in writes:
                W[nm] = [x for x in W.get(nm, []) if x[1] & ~m] + [(j, m)]
                R[nm] = [x for x in R.get(nm, []) if x[1] & ~m]
            for nm, m in reads:
                R.setdefault(nm, []).append((j, m))
            for nm, m in reads + writes:
                if nm in PSUM:
                    B.setdefault(nm, {})[q] = j
        way = [0.0] * n
        for j in range(n - 1, -1, -1):
            way[j] = calls[j][4] + calls[j][5] + max([wk + way[k] for k, wk in succ[j]] + [0.0])
        free, est, order, avail = {}, [0.0] * n, [], {}
        for j in range(n):
            if not npred[j]:
                avail.setdefault(calls[j][0], []).append(j)
        while len(order) < n:
            best = None
            for q, a in avail.items():
                if a:
                    t0 = free.get(q, 0.0)
                    s = min(max(t0, est[j]) for j in a)
                    if best is None or s < best[0]:
                        best = (s, q)
            s, q = best
            t0 = free.get(q, 0.0)
            j = max((j for j in avail[q] if max(t0, est[j]) <= s + SLACK), key=lambda j: (way[j], -j))
            soon = [i for i in avail[q] if way[i] > way[j] and s + SLACK < est[i] < s + calls[j][4] - BETA * (est[i] - s)]
            if soon:
                i = max(soon, key=lambda i: way[i])
                fit = [f for f in avail[q] if max(t0, est[f]) + calls[f][4] <= est[i] + SLACK]
                j = max(fit, key=lambda f: (way[f], -f)) if fit else i
            avail[q].remove(j)
            free[q] = max(t0, est[j]) + calls[j][4]
            order.append(j)
            for k, wk in succ[j]:
                est[k] = max(est[k], free[q] + calls[j][5] + wk)
                npred[k] -= 1
                if not npred[k]:
                    avail.setdefault(calls[k][0], []).append(k)
        for j in order:
            calls[j][1](calls[j][2], calls[j][3])

    def col(x):
        return [x] if isinstance(x, tuple) else []

    def ap(x):
        return x[0] if isinstance(x, tuple) else x

    def vcost(o, a, k=1.0):
        if len(a) > 3:
            return 0.06 + a[3] * 0.0016
        if len(o) > 3:
            return 0.06 + o[3] * 0.0035
        return max(64, wide(a) * k) * 0.00104

    def tt(o, a, b, op):
        k = 1.0 if any(x[1][0][0] in PSUM for x in (a, b)) else 2.0
        E("v", lambda: V.tensor_tensor(out=o[0], in0=a[0], in1=b[0], op=op), [a, b], [o], vcost(o, a, k))

    def ts(o, a, s1, op0, s2=None, op1=None):
        kw = dict(scalar2=None) if op1 is None else dict(scalar2=ap(s2), op1=op1)
        k = 0.5 if a[1][0][0] in TWO and o[1][0][0] in TWO else 1.0
        E("v", lambda: V.tensor_scalar(out=o[0], in0=a[0], scalar1=ap(s1), op0=op0, **kw), [a] + col(s1) + col(s2), [o], vcost(o, a, k))

    def cp(o, a):
        E("v", lambda: V.tensor_copy(out=o[0], in_=a[0]), [a], [o], vcost(o, a))

    def fill(o, c):
        E("v", lambda: V.memset(o[0], c), [], [o], vcost(o, o))

    def act(o, a, f=F.Copy, bias=0.0, scale=1.0):
        E("s", lambda: S.activation(out=o[0], in_=a[0], func=f, bias=ap(bias), scale=ap(scale)), [a] + col(bias) + col(scale), [o],
          vcost(o, a))

    def mm(o, l, r, start=True, stop=True):
        k = 4 if l[1][0][0] in BUFS[F32] else 1
        E("t", lambda: PE.matmul(out=o[0], lhsT=l[0], rhs=r[0], start=start, stop=stop), [l, r], [o], max(64, wide(r)) * k * 0.00104)

    def tr(o, a):
        E("t", lambda: PE.transpose(out=o[0], in_=a[0], identity=w("IDB")[0]), [a, w("IDB")], [o], 0.13)

    def iota(o, pat, base, cm):
        E("g", lambda: g.iota(o[0], pattern=pat, base=base, channel_multiplier=cm, allow_small_or_imprecise_dtypes=True), [], [o],
          0.15 + 0.002 * wide(o))

    def aff(o, a, pat, op, base, cm):
        E("g", lambda: g.affine_select(out=o[0], in_=a[0], pattern=pat, compare_op=op, fill=0.0, base=base, channel_multiplier=cm),
          [a], [o], 0.2 + 0.002 * wide(o))

    ALL = (1 << 1024) - 1
    dma("d", T["DET"][:, :], T.det[:, :], "ld0", [], [("DET", ALL)])
    dma("d", T["hamt"][:, :], T.ham[:, :], "ld1", [("DET", ALL)], [("hamt", (1 << 3584) - 1)])

    fill(w("ONEB"), 1.0)
    fill(w("ONE"), 1.0)
    fill(w("NEGI"), -1.0)
    fill(w("QE"), 4096.0)
    fill(w("C64"), 64.0)
    iota(w("PI"), [[-1, 16]], 16, 1)
    iota(w("PJ"), [[0, 1]], 0, 1)
    aff(w("G8"), w("ONEB", 0, 8), [[-16, 8]], O.is_ge, 0, 1)
    aff(w("G8"), w("G8"), [[16, 8]], O.is_ge, 15, -1)
    for t in range(3):
        iota(w("PK", 8 * t, 8 * t + 8), [[128, 8]], 310 * (t + 1), 1)
    aff(w("TRI"), w("ONEB", 0, 128), [[1, 128]], O.is_ge, -1, -1)
    iota(w("SW"), [[16, 16]], 1024, 0)
    iota(w("KD"), [[0, 8], [-2048, 17]], 0, 0)
    aff(w("DM"), w("ONE", 0, 136), [[-16, 8], [0, 17]], O.is_ge, 0, 1)
    aff(w("DM"), w("DM"), [[16, 8], [0, 17]], O.is_ge, 15, -1)
    aff(w("IDB"), w("ONEB", 0, 128), [[-1, 128]], O.is_equal, 0, 1)
    aff(w("QE"), w("QE"), [[-16, 8], [-2, 16]], O.is_equal, 0, 1)
    aff(w("QW"), w("ONE", 0, 128), [[-16, 8], [-2, 16]], O.is_equal, -1, 1)
    tt(w("QW"), w("QW"), w("QE"), O.add)
    aff(w("QW"), w("QW"), [[0, 8], [-1, 16]], O.is_ge, 7, 0)
    aff(w("SHP"), w("ONE", 0, 128), [[1, 128]], O.is_equal, -1, -1)
    aff(w("SHN"), w("ONE", 0, 128), [[1, 128]], O.is_equal, 1, -1)
    iota(w("KC"), [[-1, 16], [0, 8]], 15, 0)
    iota(w("SC"), [[128, 2]], 0, 1)
    iota(w("WT", 0, 8), [[-208, 8]], 5, 13)
    iota(w("WT", 8, 16), [[224, 8]], 255, -14)
    aff(w("WT", 0, 16), w("WT", 0, 16), [[0, 2], [-16, 8]], O.is_ge, 0, 1)
    aff(w("WT", 0, 16), w("WT", 0, 16), [[0, 2], [16, 8]], O.is_ge, 15, -1)
    aff(w("WT", 16, 24), w("ONE", 0, 8), [[-16, 8]], O.is_equal, -15, 1)
    ts(w("PL"), w("PK"), 1023, O.bitwise_and)
    ts(w("PA"), w("PL"), -2048.0, O.add, 0.5, O.mult)
    ts(w("PI"), w("PI"), 15, O.bitwise_and)
    ts(w("MR"), w("PI"), 0.0, O.is_equal)
    ts(w("PJ"), w("PJ"), 15, O.bitwise_and)
    cp(w("RC"), w("PJ"))
    ts(w("SW"), w("SW"), w("RC"), O.add)
    aff(w("NEGI"), w("NEGI"), [[-1, 128]], O.is_equal, 0, 1)
    for h in range(2):
        aff(w("SV%d" % h), w("C64"), [[-2, 8], [0, 16]], O.is_equal, -h, 1)
        aff(w("SK%d" % h), w("ONEB", 0, 128), [[-2, 8], [0, 16]], O.is_equal, -32 - h, 1)
        aff(w("SS%d" % h), w("ONEB", 0, 128), [[-2, 8], [0, 16]], O.is_equal, -h, 1)

    MAG = 12582912.0
    START = [310 * (t + 1) & 1023 for t in range(3)]

    def rot(t, a, b):
        s, cut = START[t], 1024 - START[t]
        out = []
        if a < cut:
            out.append((a, min(b, cut), a + s))
        if b > cut:
            out.append((max(a, cut), b, max(a, cut) - cut))
        return out

    for c in (0, 512):
        ts(w("CI", c, c + 512), w("DET", c, c + 512), 255, O.bitwise_and)
        ts(w("TC", c, c + 512), w("CI", c, c + 512), -128.0, O.add)
    for a, b in ((0, 202), (202, 714), (714, 1024)):
        for x, y, p in rot(0, a, b):
            act(w("QB", x, y), w("TC", p, p + y - x), F.Abs)
    for c in (0, 512):
        ts(w("TV", c, c + 512), w("DET", c, c + 512), -128.0, O.add, 1 / 256, O.mult)
        act(w("TM", c, c + 512), w("TV", c, c + 512), F.Identity, MAG)
        act(w("TD", c, c + 512), w("TM", c, c + 512), F.Identity, -MAG)
    fill(w("SHP", 0, 128, 16), 0.0)
    fill(w("SHN", 15, 128, 16), 0.0)
    fill(w("BIGL"), 0.0)
    fill(w("BIGL", 15, 128, 16), 64.0)
    fill(w("C128"), 1 / 128)
    fill(w("TC", 1024, 1280), 0.0)
    fill(w("TD", 1024, 1280), 0.0)
    fill(w("ZG"), 0.0)
    cp(w("ZG", 8, 16), w("G8"))
    ts(w("G16"), w("G8"), 16.0 * 37, O.mult)
    SEL = [w("ZG", 8, 24), w("ZG", 0, 16)]

    for h in range(2):
        aff(w("SVX%d" % h), w("ONEB", 0, 128), [[-2, 8], [0, 16]], O.is_equal, -16 - h, 1)
    iota(w("TRS"), [[0, 8], [128, 2]], 256, 1)
    iota(w("TRA"), [[0, 8], [128, 2]], 1024, 1)
    iota(w("MC"), [[1, 10], [0, 16]], 2048, 0)
    iota(w("IM"), [[1, 10], [0, 16]], 0, 0)
    iota(w("XI"), [[16, 8]], 0, 0)
    iota(w("XJ"), [[0, 1]], 0, 1)
    aff(w("SEL8"), w("ONEB", 0, 8), [[-16, 8]], O.is_equal, -8, 1)
    aff(w("RW"), w("G8"), [[16, 8]], O.is_ge, 7, -1)
    for h in range(2):
        z = w("ZW", 640 * h + 160, 640 * h + 320)
        aff(z, w("ONEB", 0, 160), [[0, 10], [-16, 16]], O.is_ge, 128 * h, 1)
        aff(z, z, [[0, 10], [16, 16]], O.is_ge, 15 - 128 * h, -1)

    def late_constants():
        for h in range(2):
            tt(w("SV%d" % h), w("SV%d" % h), w("SVX%d" % h), O.add)
        fill(w("R8"), 0.0)
        cp(w("R8", 8, 128, 16), w("G8"))
        ts(w("B1"), w("RC"), -8192.0, O.mult, 8192.0 * 15 + 4096, O.add)
        ts(w("B2"), w("RC"), 8192.0, O.mult, 4096 - 8192.0 * 15, O.add)
        for t in range(3):
            fill(w("SB%d" % t, 0, 256), 0.0)

    def last_constants():
        ts(w("SELB"), w("SEL8"), 16.0, O.mult)
        tt(w("RW"), w("RW"), w("SELB"), O.add)
        for h in range(2):
            z = [w("ZW", 640 * h + 160 * f, 640 * h + 160 * f + 160) for f in range(4)]
            ts(z[0], z[1], 32.0, O.mult)
            tt(z[3], z[1], w("IM"), O.mult)
            ts(z[2], z[3], 32.0, O.mult)
        ts(w("XI"), w("XI"), w("RC"), O.add)
        L3 = math.log(3.0)
        ts(w("XI"), w("XI"), -L3, O.mult, 55 * L3, O.add)
        ts(w("XJ"), w("XJ"), -L3, O.mult, 55 * L3, O.add)
        act(w("WX"), w("XI"), F.Exp)
        act(w("THR"), w("XJ"), F.Exp)
        ts(w("THR"), w("THR"), 2.2, O.mult)
        for c in range(8):
            ts(w("WC", 8 * c, 8 * c + 8), w("G8"), w("WX", c, c + 1), O.mult)
        ts(w("WBIG"), w("G8"), 1e29, O.mult)
        ts(w("IDN"), w("IDB"), -1 / 256, O.mult)

    def t2w(src, n, X):
        for r in range(16):
            if r % 2:
                act(w(X, r, 16 * n, 16), src, F.Copy, 0.0, w("MR", r, r + 1))
            else:
                ts(w(X, r, 16 * n, 16), src, w("MR", r, r + 1), O.mult)

    peers = [q for q in range(4) if q != me]
    near = [q for q in peers if T.cores[q] in topo.cores_of(core)]
    far = [q for q in peers if q not in near]

    def send(t):
        sb, plan, used, share = "SB%d" % t, [], [], []
        for i, q in enumerate(far):
            e = topo.engines(core, T.cores[q])
            k = len(e) // len(far)
            share.append(k)
            plan.append((q, e[i * k:(i + 1) * k]))
            used += e[i * k:(i + 1) * k]
        for i, q in enumerate(near):
            e = [x for x in topo.engines(core, T.cores[q]) if x not in used]
            k = min([len(e) // len(near)] + share)
            plan.append((q, e[i * k:(i + 1) * k]))
        got = sum(len(e) for q, e in plan)
        rx = "rx%d" % t

        def emit(reads, writes):
            deps("g", reads, [])
            tf = []
            for q, e in plan:
                rid, pid = topo.addr(T.cores[q], core)
                tf.append(RemoteDMATransfer(dst_ids=[DstId(rid=rid, pnc=pid)], dma_engine_mask=sum(1 << x for x in e),
                                            remote_sem=T.sem[rx], src=T[sb][:, 64 * q:64 * q + 64],
                                            dst=T["IN%d" % t][:, 64 * me:64 * me + 64], alu_op=0))
            g.remote_dma_fused(tf, local_sem=T.sem["snd"])
            semof[rx] = (rx, got)
            note(rx, 1, [], writes)
        calls.append(("g", emit, w(sb, 0, 256)[1], [r for q in peers for r in w("IN%d" % t, 64 * q, 64 * q + 64)[1]], 0.5, 4.0))
        act(w("IN%d" % t, 64 * me, 64 * me + 64), w(sb, 64 * me, 64 * me + 64))
        return got

    def first_qt(b):
        mm(w("P6", 0, 512), w("QW"), w("TD", 512 * b, 512 * b + 512), True, False)
        parts = [(0, 310, 714), (310, 512, 0)] if b == 0 else [(0, 512, 202)]
        for i, (x, y, p) in enumerate(parts):
            mm(w("P6", x, y), w("R8"), w("QB", p, p + y - x), False, i == len(parts) - 1)
        act(w("QT", 512 * b, 512 * b + 512), w("P6", 0, 512))

    sent = 0
    for t in range(3):
        IN, SB = "IN%d" % t, "SB%d" % t
        if t:
            for a in range(0, 1024, 256):
                for x, y, p in rot(t, a, a + 256):
                    act(w("QB", x, y), w("QT", p, p + y - x))
        for k in range(8):
            mm(w("P0", 8 * k, 8 * k + 8), w("QB", 128 * k, 128 * k + 128), w("SEL8") if t else w("G8"))
        ts(w("LV"), w("P0", 0, 64), 0.0, O.is_gt)
        ts(w("DB"), w("P0", 0, 64), 0.0, O.is_equal, 4096.0, O.mult)
        mm(w("P1", 0, 64), w("TRI"), w("LV"), True, False)
        for d in range(1, 8):
            mm(w("P1", 8 * d, 64), w("ONEB", 0, 128), w("LV", 0, 64 - 8 * d), False, d == 7)
        tt(w("RF"), w("P1", 0, 64), w("DB"), O.add)
        tt(w("R32"), w("P1", 0, 64), w("DB"), O.add)
        ts(w("LOW"), w("R32"), 15, O.bitwise_and)
        for h in range(17):
            act(w("BS", h, 1088, 17), w("RF"), F.Sign, 0.5 - 16 * h)
        if t == 0:
            late_constants()
        for l in range(16):
            ts(w("OL", l, 1024, 16), w("LOW"), float(l), O.is_equal)
        for k in range(8):
            c = (128 * k, 128 * k + 128)
            ts(w("OA", *c), w("OL", *c), w("PA", 8 * t + k, 8 * t + k + 1), O.mult)
        mm(w("P2", 0, 136), w("C128"), w("KD"), True, False)
        for k in range(8):
            mm(w("P2", 0, 136), w("OA", 128 * k, 128 * k + 128), w("BS", 136 * k, 136 * k + 136), False, k == 7)
        for k in range(8):
            mm(w("P0", 0, 8), w("ONEB", 0, 128), w("LV", 8 * k, 8 * k + 8), k == 0, k == 7)
        if t:
            cp(ind(w("TD"), w("FO")), w("AD"))
        tt(w("LM"), w("P2", 0, 136), w("DM"), O.mult)
        for n in (68, 34, 17):
            tt(w("LM", 0, n), w("LM", 0, n), w("LM", n, 2 * n), O.add)
        tt(w("LD"), w("LM", 0, 16), w("LM", 1, 17), O.subtract)
        tt(w("GU"), w("LD"), w("SW"), O.min)
        act(w("AB"), ind(w("TC"), w("GU")), F.Abs)
        mm(w("P3", 0, 256), w("IDB"), w("AB"))
        cp(w("DU"), ind(w("TD"), w("GU")))
        CUT = [0, 64, 128, 192, 256]

        def look(a, b):
            return w("hv", 16 * a, 16 * b), ind(w("hamt"), w("DU", a, b))
        for j in range(1, 4):
            act(*look(CUT[j], CUT[j + 1]))
        act(w("CN"), ind(w("TC"), w("GU")))
        cp(w("DF"), w("DU"))
        cp(*look(CUT[0], CUT[1]))
        for h in range(2):
            mm(w("P0", 64 + h, 96, 2), w("DF", 128 * h, 128 * h + 128), w("WT", 0, 16))

        def mins(a, b):
            for k in list(range(8, 16)) + list(range(8)):
                tt(w("MK", 256 * k + a, 256 * k + b), w("hv", 16 * a + k, 16 * b, 16), w("P3", a, b), O.min)

        UP = ["P1", "P6"]

        def tree(h):
            for p, ks in ((UP[h], range(8, 16)), ("P%d" % (1 + h), range(8))):
                mm(w(p, 8 * ks[0], 8 * ks[0] + 64), w("C128"), w("KC", 8 * ks[0], 8 * ks[0] + 64), True, False)
                for k in ks:
                    mm(w(p, 8 * k, 8 * k + 8), w("MK", 256 * k + 128 * h, 256 * k + 128 * h + 128), w("G16"), False, k == ks[-1])
            cp(w("EM" if h else "EU"), w(UP[h], 64, 128))

        def top(h):
            p, o = "P%d" % (1 + h), 128 * h
            tt(w("ET", o, o + 64), w(p, 0, 64), w("EM" if h else "EU"), O.max)
            for n in (32, 16):
                tt(w("ET", o, o + n), w("ET", o, o + n), w("ET", o + n, o + 2 * n), O.max)
            tt(w("MX", h, 16, 2), w("ET", o, o + 8), w("ET", o + 8, o + 16), O.max)
        mm(w("P4", 0, 256), w("SHP"), w("DF"))
        mm(w("P4", 256, 512), w("SHN"), w("DF"), True, False)
        mm(w("P4", 256, 512), w("BIGL"), w("ONEB"), False, True)
        mm(w("P5", 0, 256), w("NEGI"), w("DF"), True, False)
        act(w("DP"), w("P4", 0, 256))
        act(w("DN"), w("P4", 256, 512))
        if t == 0:
            first_qt(0)
        mins(0, CUT[2])
        tree(0)
        mins(CUT[2], CUT[3])
        for h in range(2):
            ts(w("ON", h, 16, 2), w("P0", 0, 8), w("SC", h, h + 1), O.is_gt)
        cp(w("H1"), w("P0", 64, 96))
        ts(w("H2"), w("H1"), 4095, O.bitwise_and)
        tt(w("HP"), w("H2", 0, 16), w("H2", 16, 32), O.mult)
        ts(w("HP"), w("HP"), 5, O.arith_shift_right)
        ts(w("HV"), w("HP"), 16.0, O.mult, 16.0 * t, O.add)
        top(0)
        mins(CUT[3], CUT[4])
        tree(1)
        top(1)
        ts(w("F4", 32, 48), w("MX"), 15, O.bitwise_and)
        tt(w("E3"), w("MX"), w("HV"), O.add)
        ts(w("F4", 0, 16), w("E3"), 10, O.arith_shift_right, 63, O.bitwise_and)
        ts(w("F4", 16, 32), w("E3"), 4, O.arith_shift_right, 63, O.bitwise_and)
        cp(w("F4B"), w("F4"))
        tr(w("TP", 0, 128, 1, 48), w("F4B"))
        r4 = w("R4", 0, 128, 1, 48)
        cp(r4, w("TP", 0, 128, 1, 48))
        for h in range(2):
            mm(w("P2", 128 * h, 128 * h + 128), w("SK%d" % h, 0, 128, 1, 48), r4)
        for h in range(2):
            mm(w("P6", 128 * h, 128 * h + 128), w("SV%d" % h, 0, 128, 1, 48), r4)
        for h in range(2):
            mm(w("P5", 128 * h, 128 * h + 128), w("SV%d" % h, 0, 128, 1, 48), r4, False, h == 1)
        act(w("P0", 0, 256), w("P2", 0, 256), F.Relu, w("B2"), 8192.0)
        act(w("P1", 0, 256), w("P2", 0, 256), F.Relu, w("B1"), -8192.0)
        act(w("SG"), w("P5", 0, 256), F.Sign)
        ts(w("FI"), w("CN"), 0.25, O.mult, -0.375, O.add)
        ts(w("KM2"), w("F4", 32, 48), 2.0, O.mult)
        ts(w("KM1"), w("F4", 32, 48), 1.0, O.add)
        ts(w("VV"), w("E3"), 4, O.arith_shift_right, 4095, O.bitwise_and)
        ts(w("OK1"), w("VV"), 3584.0, O.is_lt)
        tt(w("OK1"), w("OK1"), w("ON"), O.mult)
        tt(w("EB"), w("DN"), w("P6", 0, 256), O.min)
        tt(w("P0", 0, 256), w("DF"), w("P0", 0, 256), O.add)
        tt(w("P1", 0, 256), w("DF"), w("P1", 0, 256), O.subtract)
        tt(w("EC"), w("EB"), w("P0", 0, 256), O.min)
        tt(w("P1", 0, 256), w("DP"), w("P1", 0, 256), O.max)
        tt(w("CH"), w("EC"), w("P1", 0, 256), O.max)
        for h in range(2):
            mm(w("P3", h, 16, 2), w("SG", 128 * h, 128 * h + 128), w("G8"))
        for h in range(2):
            mm(w("P2", h, 32, 2), w("CH", 128 * h, 128 * h + 128), w("WT", 0, 16))
        act(w("P4", 0, 256), w("CH"), F.Copy, 0.0, 256.0)
        cp(w("SGI"), w("P3", 0, 16))
        tt(w("N1"), w("SGI"), w("KM2"), O.add)
        ts(w("N2"), w("N1"), 14.0, O.is_gt)
        ts(w("N4"), w("SGI"), 1, O.arith_shift_right)
        tt(w("N5"), w("N4"), w("KM1"), O.add)
        tt(w("N6"), w("N5"), w("N2"), O.add)
        ts(w("N7"), w("N6"), 1, O.bitwise_and)
        ts(w("SNB"), w("N7"), -2.0, O.mult, 1.0, O.add)
        tr(w("TP", 0, 128, 1, 16), w("SNB"))
        ts(w("N3"), w("SGI"), 1, O.bitwise_and)
        ts(w("SN0"), w("N3"), 0.0, O.is_equal)
        tt(w("OK1"), w("OK1"), w("SN0"), O.mult)
        for q in range(4):
            ts(w("QQ", 16 * q, 16 * q + 16), w("OK1"), -8.0, O.mult, 8.0 + q, O.add)
        cp(w("R5", 0, 128, 1, 16), w("TP", 0, 128, 1, 16))
        for h in range(2):
            mm(w("P0", 128 * h, 128 * h + 128), w("SS%d" % h, 0, 128, 1, 16), w("R5", 0, 128, 1, 16))
        cp(w("I1"), w("P2", 0, 32))
        ts(w("I2"), w("I1"), 4095, O.bitwise_and)
        tt(w("PR"), w("I2", 0, 16), w("I2", 16, 32), O.mult)
        ts(w("OW"), w("PR"), 5, O.arith_shift_right, 3, O.bitwise_and)
        for q in range(4):
            tt(w("OM", 16 * q, 16 * q + 16), w("OW"), w("QQ", 16 * q, 16 * q + 16), O.is_equal)
        mm(w("P5", 0, 64), w("TRI"), w("OM"), True, False)
        for q in range(4):
            mm(w("P5", 16 * q + 1, 16 * q + 16, 2), w("ONEB", 0, 128), w("OM", 16 * q, 16 * q + 16, 2), False, q == 3)
        tt(w("CF32"), w("FI"), w("P0", 0, 256), O.mult)
        for q in range(4):
            ts(w("K1", 16 * q, 16 * q + 16), w("OM", 16 * q, 16 * q + 16), -4096.0, O.mult, 4096.0 + 64 * q, O.add)
        ts(w("K5"), w("P5", 0, 64), 64.0, O.is_ge, 4096.0, O.mult)
        tt(w("K6"), w("P5", 0, 64), w("K1"), O.add)
        tt(w("K7"), w("K5"), w("K6"), O.add)
        tt(w("K2"), w("K7", 0, 32), w("K7", 32, 64), O.min)
        tt(w("K8"), w("K2", 0, 16), w("K2", 16, 32), O.min)
        for h in range(2):
            tt(w("FS", 8 * h, 8 * h + 8), w("K8", h, 16, 2), w("TRS", h, 16, 2), O.min)
        t2w(w("FS"), 16, "XF")
        for h in range(2):
            mm(w("P6", 0, 16), w("XF", 128 * h, 128 * h + 128), SEL[h], h == 0, h == 1)
        tt(w("ED"), w("CF32"), w("P4", 0, 256), O.add)
        cp(w("OFF"), w("P6", 0, 16))
        cp(ind(w(SB), w("OFF")), w("ED"))
        sent += send(t)
        act(w("P3", 256, 512), w("CN"), F.Sign)
        if t == 0:
            first_qt(1)
        tt(w("CFD"), w("CN"), w("P3", 256, 512), O.subtract)
        act(w("ABF"), w("CFD"), F.Abs)
        mm(w("P0", 0, 256), w("QW"), w("DF"), True, False)
        mm(w("P0", 0, 256), w("R8"), w("ABF"), False, True)
        act(w("QS"), w("P0", 0, 256))
        cp(ind(w("TC"), w("GU")), w("CFD"))
        if t == 0:
            last_constants()
        cp(ind(w("QT"), w("GU")), w("QS"))
        if t == 2:
            for b in range(2):
                mm(w("P5", 0, 512), w("NEGI"), w("TD", 512 * b, 512 * b + 512), True, False)
                mm(w("P5", 0, 512), w("IDN"), w("TC", 512 * b, 512 * b + 512), False, True)
                act(w("YT", 512 * b, 512 * b + 512), w("P5", 0, 512), F.Copy, 128.0, -256.0)
        ts(w("AT", 0, 128), w(IN, 0, 128), 1 / 256, O.mult, MAG, O.add)
        act(w("AT", 128, 256), w(IN, 128, 256), F.Identity, MAG, 1 / 256)
        ts(w("AD", 0, 128), w("AT", 0, 128), -MAG, O.add)
        act(w("AD", 128, 256), w("AT", 128, 256), F.Identity, -MAG)
        for h in range(2):
            mm(w("P1", h, 48, 2), w("AD", 128 * h, 128 * h + 128), w("WT"))
        mm(w("P2", 0, 256), w("QW"), w("AD"))
        act(w("P6", 0, 256), w("AD"), F.Copy, 0.0, -256.0)
        cp(w("J1"), w("P1", 0, 48))
        ts(w("J2"), w("J1", 0, 32), 4095, O.bitwise_and)
        tt(w("JP"), w("J2", 0, 16), w("J2", 16, 32), O.mult)
        ts(w("ZD", 32, 48), w("J2", 0, 16), 4, O.arith_shift_right, 31, O.bitwise_and)
        ts(w("SL2"), w("J2", 0, 16), 15, O.bitwise_and)
        ts(w("ZD", 0, 16), w("JP"), 12, O.arith_shift_right, 31, O.bitwise_and)
        ts(w("ZD", 16, 32), w("JP"), 7, O.arith_shift_right, 31, O.bitwise_and)
        ts(w("ZD", 48, 64), w("SL2"), 2.0, O.mult, 1.0, O.add)
        for h in range(2):
            cp(w("ZF", 32 * h, 32 * h + 32), w("ZD", h, 64, 2))
        t2w(w("ZF"), 64, "XB")
        act(w("QA"), w("P2", 0, 256))
        ts(w("HQ"), w("JP"), 7, O.arith_shift_right, 1023, O.bitwise_and)
        ts(w("ST0"), w("J2", 0, 16), 511, O.bitwise_and)
        ts(w("ST"), w("ST0"), 2.0, O.mult, 1.0, O.add)
        ts(w("NU"), w("J1", 32, 48), 1.0, O.is_lt, 4096.0, O.mult)
        tt(w("P6", 0, 256), w(IN), w("P6", 0, 256), O.add)
        for c in range(2):
            for h in range(2):
                for f in range(4):
                    mm(w("P%d" % (3 + c), 0, 80), w("XB", (32 * h + 8 * f) * 16, (32 * h + 8 * f) * 16 + 128),
                       w("ZW", 640 * h + 160 * f + 80 * c, 640 * h + 160 * f + 80 * c + 80), h + f == 0, h + f == 4)
            z = (80 * c, 80 * c + 80)
            cp(w("ZI", *z), w("P%d" % (3 + c), 0, 80))
            ts(w("ZJ", *z), w("ZI", *z), 1023, O.bitwise_and)
            cp(w("ZU", *z), w("ZJ", *z))
        SCP = ["P5", "P0", "P1"]

        def probe(m):
            o = w("CMP", 256 * m, 256 * m + 256)
            if m < 4:
                tt(o, ind(w("QT", 0, 1024), w("ZU", 16 * m, 16 * m + 16)), w("QA"), O.is_equal)
            else:
                tt(o, w("PR5", 256 * (m - 4), 256 * (m - 3)), w("P2", 0, 256), O.is_equal)
            for h in range(2):
                mm(w(SCP[0 if m < 5 else 1 if m < 8 else 2], 16 * (m % 5) + h, 16 * (m % 5) + 16, 2),
                   w("CMP", 256 * m + 128 * h, 256 * m + 128 * h + 128), w("RW"))

        def score(c):
            a, b = ((0, 5), (5, 8), (8, 10))[c]
            p, z = w(SCP[c], 16 * (a % 5), 16 * (b - 1) % 80 + 16), (16 * a, 16 * b)
            ts(w("S2", *z), p, 8.0, O.is_ge, -1024.0, O.mult)
            ts(p, p, 8.0, O.is_equal, -1024.0, O.mult)
            tt(w("S3", *z), w("S2", *z), w("MC", *z), O.add)
            tt(w("S1", *z), p, w("S3", *z), O.add)
        for m in range(6):
            act(w("PR5", 256 * m, 256 * m + 256), ind(w("QT", 0, 1024), w("ZU", 16 * m + 64, 16 * m + 80)))
        for m in range(6):
            probe(m)
        score(0)
        tt(w("S4", 0, 32), w("S1", 0, 32), w("S1", 32, 64), O.min)
        tt(w("S5", 0, 16), w("S4", 0, 16), w("S4", 16, 32), O.min)
        tt(w("S6"), w("S5", 0, 16), w("S1", 64, 80), O.min)
        for m in (6, 7):
            probe(m)
        score(1)
        tt(w("S4", 32, 48), w("S1", 80, 96), w("S1", 96, 112), O.min)
        tt(w("S5", 16, 32), w("S4", 32, 48), w("S1", 112, 128), O.min)
        tt(w("S4", 48, 64), w("S5", 16, 32), w("S6"), O.min)
        for m in (8, 9):
            probe(m)
        score(2)
        tt(w("S4", 64, 80), w("S1", 128, 144), w("S1", 144, 160), O.min)
        tt(w("S7"), w("S4", 64, 80), w("S4", 48, 64), O.min)
        tt(w("M3"), w("S7"), w("ST"), O.mult)
        tt(w("SN"), w("S7"), w("NU"), O.add)
        ts(w("M4"), w("SN"), 2048.0, O.is_ge, 2048.0, O.mult)
        ts(w("M5"), w("SN"), 2048.0, O.is_ge, 32.0, O.mult)
        tt(w("PN"), w("M3"), w("HQ"), O.add)
        ts(w("DG", 0, 16), w("PN"), 6, O.arith_shift_right, 15, O.bitwise_and)
        ts(w("DG", 16, 32), w("PN"), 63, O.bitwise_and)
        tt(w("FD", 0, 16), w("DG", 0, 16), w("M5"), O.add)
        cp(w("FD", 16, 32), w("DG", 16, 32))
        ts(w("PM"), w("PN"), 1023, O.bitwise_and)
        tt(w("PLC"), w("PM"), w("M4"), O.add)
        tt(w("PT"), w("PLC"), w("TRA"), O.min)
        tr(w("TP", 0, 128, 1, 32), w("FD"))
        for h in range(2):
            cp(w("PF", 8 * h, 8 * h + 8), w("PLC", h, 16, 2))
        cp(w("R6", 0, 128, 1, 32), w("TP", 0, 128, 1, 32))
        for h in range(2):
            mm(w("P0", 128 * h, 128 * h + 128), w("SV%d" % h, 0, 128, 1, 32), w("R6", 0, 128, 1, 32))
        t2w(w("PF", 0, 16), 16, "XF")
        for h in range(2):
            mm(w("P1", 0, 16), w("XF", 128 * h, 128 * h + 128), SEL[h], h == 0, h == 1)
        cp(w("PU"), w("P0", 0, 256))
        cp(w("PW"), w("P1", 0, 16))
        ts(w("PO"), w("PW"), 1279.0, O.min)
        act(w("CO"), ind(w("TC"), w("PO")))
        if t == 2:
            act(w("P1", 0, 256), w("AD"), F.Copy, 128.0, 256.0)
        tt(w("CV"), w("CO"), w("P6", 0, 256), O.add)
        ts(w("CNW"), w("CV"), 127.0, O.min, -127.0, O.max)
        if t < 2:
            act(w("ABN"), w("CNW"), F.Abs)
            mm(w("P2", 0, 256), w("R8"), w("ABN"))
            tt(w("QN"), w("QA"), w("P2", 0, 256), O.add)
        else:
            tt(w("YN"), w("CNW"), w("P1", 0, 256), O.add)
        for c in range(16):
            a = 0 if c < 8 else 128
            ts(w("MK", 256 * c + a, 256 * c + 256), w("PU", a, 256), w("PW", c, c + 1), O.is_equal)
            wc = w("WC", 8 * (c % 8), 8 * (c % 8) + 8)
            if c < 8:
                mm(w("P3", 0, 16, 2), w("MK", 256 * c, 256 * c + 128), wc, c == 0, c == 7)
            mm(w("P4", 1, 16, 2), w("MK", 256 * c + 128, 256 * c + 256), wc if c > 7 else w("WBIG"), c == 0, c == 15)
        for h in range(2):
            ts(w("LO", h, 16, 2), w("P%d" % (3 + h), h, 16, 2), w("THR"), O.is_ge, w("TRA", h, h + 1), O.mult)
        for h in range(2):
            tt(w("PF", 16 + 8 * h, 24 + 8 * h), w("LO", h, 16, 2), w("PT", h, 16, 2), O.max)
        t2w(w("PF", 16, 32), 16, "XF")
        for h in range(2):
            mm(w("P5", 0, 16), w("XF", 128 * h, 128 * h + 128), SEL[h], h == 0, h == 1)
        cp(w("FO"), w("P5", 0, 16))
        if t < 2:
            cp(ind(w("QT"), w("FO")), w("QN"))
            cp(ind(w("TC"), w("FO")), w("CNW"))
        else:
            cp(ind(w("YT"), w("FO")), w("YN"))
            dma("d", T.y[:, :], T["YT"][:, 0:1024], "st0", w("YT", 0, 1024)[1], [])
    schedule()
    wait("d", "st0", 1)
    g.wait_ge(T.sem.snd, sent)
    for q in ("v", "s", "t", "g"):
        wait("g", q, cnt[q])
